import numpy as np
import ml_dtypes


def mxq(x, axis, fmt="e4m3"):
    dtype, down = {"e4m3": (ml_dtypes.float8_e4m3fn, 7), "e5m2": (ml_dtypes.float8_e5m2, 14)}[fmt]
    v = np.moveaxis(np.asarray(x, np.float32).astype(ml_dtypes.bfloat16).astype(np.float64), axis, -1)
    blocks = v.reshape(v.shape[:-1] + (-1, 32))
    amax = np.abs(blocks).max(-1, keepdims=True)
    byte = np.maximum(np.where(amax > 0, np.frexp(amax)[1] - 1 + 127, 0) - down, 1)
    scale = np.exp2(byte - 127.0)
    codes = (blocks / scale).astype(np.float32).astype(dtype).astype(np.float64)
    return np.moveaxis((codes * scale).reshape(v.shape), -1, axis)


WIDE = False


def mx_kscale(k):
    if not WIDE:
        return np.ones(k)
    levels = np.array([10, -10, 5, -5, 0])
    if k % 512:
        return np.exp2(np.random.permutation(np.resize(levels, k // 32))).repeat(32)
    a = np.empty((k // 512, 16))
    for p in range(k // 512):
        a[p, :8] = np.random.permutation(np.resize(levels, 8))
        for g in range(8):
            far = levels[np.abs(levels - a[p, g]) >= 10]
            a[p, g + 8] = far[np.random.randint(len(far))]
    return np.exp2(a.ravel()).repeat(32)


def f64(x):
    return np.asarray(x).astype(np.float64)


E2M1 = np.array([0.0, 0.5, 1.0, 1.5, 2.0, 3.0, 4.0, 6.0, -0.0, -0.5, -1.0, -1.5, -2.0, -3.0, -4.0, -6.0])


def pack_weight(w, fmt):
    k, n = w.shape
    w = f64(np.asarray(w, np.float32).astype(ml_dtypes.bfloat16)).reshape(k // 32, 32, n)
    amax = np.abs(w).max(1)
    if fmt == "e4m3":
        byte = np.frexp(amax)[1] - 1 + 127 - 7
    else:
        mant, ex = np.frexp(amax / 6.0)
        byte = np.where(mant > 0.5, ex, ex - 1) + 127
    byte = np.clip(np.where(amax > 0, byte, 1), 1, 254)
    scaled = (w * np.exp2(127.0 - byte)[:, None, :]).reshape(k, n).astype(np.float32)
    by_word = np.ascontiguousarray(scaled.reshape(k // 512, 128, 4, n).transpose(0, 1, 3, 2))
    if fmt == "e4m3":
        words = by_word.astype(ml_dtypes.float8_e4m3fn).view(np.uint8)
    else:
        c = by_word.astype(ml_dtypes.float4_e2m1fn).view(np.uint8) & 0xF
        words = (c[..., 0::2] | (c[..., 1::2] << 4)).reshape(k // 512, 128, 2 * n)
    return np.ascontiguousarray(words), np.ascontiguousarray(byte.astype(np.uint8).reshape(k // 512, 16, n))


def unpack_weight(words, scales, fmt):
    g, _, n = scales.shape
    words = np.ascontiguousarray(words).reshape(g, 128, n, -1)
    if fmt == "e4m3":
        vals = words.view(ml_dtypes.float8_e4m3fn).astype(np.float64)
    else:
        nib = np.empty((g, 128, n, 4), np.uint8)
        nib[..., 0::2] = words & 0xF
        nib[..., 1::2] = words >> 4
        vals = E2M1[nib]
    vals = vals * np.repeat(np.exp2(scales.astype(np.float64) - 127.0), 8, axis=1)[..., None]
    return vals.transpose(0, 1, 3, 2).reshape(g * 512, n)


K, M, T = 1536, 512, 1024


def setup_inputs():
    n = np.random.standard_normal
    s = mx_kscale(K)[:, None]
    x = n((K, T)) * s
    x4 = pack_weight(x, "e2m1")
    rest = x - unpack_weight(*x4, "e2m1")
    p_w4 = pack_weight(n((K, M)) / np.sqrt(K) / s, "e2m1")
    return {
        "x4_words": x4[0],
        "x4_scales": x4[1],
        "xr": (rest).astype(np.float32),
        "w4_words": p_w4[0],
        "w4_scales": p_w4[1],
    }


def reference(x4_words, x4_scales, xr, w4_words, w4_scales):
    x4_ = unpack_weight(x4_words, x4_scales, "e2m1")
    xr_ = mxq(f64(xr), 0, "e4m3")
    w4_ = unpack_weight(w4_words, w4_scales, "e2m1")
    y = x4_.T @ w4_ + xr_.T @ w4_
    return np.maximum(y, 0.0) ** 2

@@ -1,0 +1,194 @@
+from contextlib import ExitStack
+
+import concourse.mybir as mybir
+
+K, T, N = 1536, 1024, 512
+FLOPS = 2 * 2 * K * T * N
+
+F32 = mybir.dt.float32
+BF16 = mybir.dt.bfloat16
+I32 = mybir.dt.int32
+U32 = mybir.dt.uint32
+U8 = mybir.dt.uint8
+FP8X4 = mybir.dt.float8_e4m3fn_x4
+FP4X4 = mybir.dt.float4_e2m1fn_x4
+ACT = mybir.ActivationFunctionType
+
+P = 128
+PASSES = K // 512
+TILES = T // P
+
+
+def tile_mix_xres_tm_relu2_kernel(tc, x4_words, x4_scales, xr, w4_words, w4_scales, out):
+    nc = tc.nc
+    with ExitStack() as ctx:
+        keep = ctx.enter_context(tc.tile_pool(name="keep", bufs=1))
+        psum = ctx.enter_context(tc.psum_pool(name="psum", bufs=1))
+        ctx.enter_context(tc.manual_schedule())
+
+        w4 = keep.tile([P, PASSES, 2 * N], U8, name="w4", align_bytes=64)
+        w4s = keep.tile([P, PASSES, N], U8, name="w4s", align_bytes=64)
+        x4 = keep.tile([P, PASSES, 2 * T], U8, name="x4", align_bytes=64)
+        x4s = keep.tile([P, PASSES, T], U8, name="x4s", align_bytes=64)
+        bf = [keep.tile([P, T, 4], BF16, name=f"bf{a}", align_bytes=64) for a in range(PASSES)]
+        codes = [keep.tile([P, T], U32, name=f"codes{a}", align_bytes=64) for a in range(PASSES)]
+        scales = [keep.tile([P, T], U8, name=f"scales{a}", align_bytes=64) for a in range(PASSES)]
+        rel = [keep.tile([P, N], F32, name=f"rel{i}", align_bytes=64) for i in range(TILES)]
+        res = [keep.tile([P, N], F32, name=f"res{i}", align_bytes=64) for i in range(TILES)]
+        warm = keep.tile([P, 1], F32, name="warm")
+        acc = [psum.tile([P, N], F32, name=f"acc{i}") for i in range(TILES)]
+
+        nc.vector.memset(w4s[:].rearrange("p a n -> p (a n)").bitcast(I32), 0)
+        nc.vector.memset(x4s[:].rearrange("p a n -> p (a n)").bitcast(I32), 0)
+        nc.gpsimd.memset(warm[:], 0.0)
+
+        def load_words(tile, words):
+            nc.sync.dma_start(out=tile[:].bitcast(I32), in_=words.rearrange("a p n -> p a n").bitcast(I32))
+
+        def load_scales(tile, rows):
+            for q in range(4):
+                nc.sync.dma_start(
+                    out=tile[:].bitcast(I32)[32 * q : 32 * q + 4, :, :],
+                    in_=rows[:, 4 * q : 4 * q + 4, :].rearrange("a r n -> r a n").bitcast(I32),
+                )
+
+        raw = {}
+
+        def load_xr(a, i0, i1):
+            tile = keep.tile([P, 4, P * (i1 - i0)], F32, name=f"raw{a}_{i0}", align_bytes=64)
+            rows = xr[512 * a : 512 * (a + 1), P * i0 : P * i1]
+            nc.sync.dma_start(out=tile[:], in_=rows.rearrange("(p j) t -> p j t", j=4))
+            for i in range(i0, i1):
+                raw[a, i] = (tile, P * (i - i0))
+
+        def copy(engine_copy, a, i0, i1):
+            tile, t0 = raw[a, i0]
+            engine_copy(
+                out=bf[a][:, P * i0 : P * i1, :].rearrange("p (c i) j -> p c j i", i=4),
+                in_=tile[:, :, t0 : t0 + P * (i1 - i0)].rearrange("p j (c i) -> p c j i", i=4),
+            )
+
+        def v_copy(a, i0, i1):
+            copy(nc.vector.tensor_copy, a, i0, i1)
+
+        def s_copy(a, i0, i1):
+            copy(nc.scalar.copy, a, i0, i1)
+
+        def quant(a, i0, i1):
+            cols = slice(P * i0, P * i1)
+            nc.vector.quantize_mx(
+                out=codes[a][:, cols].bitcast(FP8X4),
+                scales=scales[a][:, cols],
+                in_=bf[a][:, cols, :].rearrange("p t j -> p (t j)"),
+            )
+            for i in range(i0, i1):
+                mm_xr(a, i)
+
+        def mm_x4(i):
+            for a in range(PASSES):
+                nc.tensor.matmul_mx(
+                    out=acc[i][:],
+                    lhsT=x4[:, a, 2 * P * i : 2 * P * (i + 1)].bitcast(FP4X4),
+                    lhsT_scale=x4s[:, a, P * i : P * (i + 1)],
+                    rhs=w4[:, a, :].bitcast(FP4X4),
+                    rhs_scale=w4s[:, a, :],
+                    start=(a == 0 and i >= 4),
+                    stop=False,
+                )
+
+        def mm_xr(a, i):
+            nc.tensor.matmul_mx(
+                out=acc[i][:],
+                lhsT=codes[a][:, P * i : P * (i + 1)].bitcast(FP8X4),
+                lhsT_scale=scales[a][:, P * i : P * (i + 1)],
+                rhs=w4[:, a, :].bitcast(FP4X4),
+                rhs_scale=w4s[:, a, :],
+                start=(a == 0 and i < 4),
+                stop=(a == PASSES - 1),
+            )
+
+        def relu(i, cols=slice(0, N)):
+            nc.scalar.activation(out=rel[i][:, cols], in_=acc[i][:, cols], func=ACT.Relu)
+
+        def v_square(i, cols=slice(0, N)):
+            nc.vector.tensor_mul(out=res[i][:, cols], in0=rel[i][:, cols], in1=rel[i][:, cols])
+
+        def s_square(i, cols=slice(0, N)):
+            nc.scalar.activation(out=res[i][:, cols], in_=rel[i][:, cols], func=ACT.Square)
+
+        def store(i, cols=slice(0, N)):
+            nc.sync.dma_start(out=out[P * i : P * (i + 1), cols], in_=res[i][:, cols])
+
+        nc.scalar.activation(out=warm[:], in_=warm[:], func=ACT.Relu)
+        load_words(w4, w4_words)
+        load_scales(w4s, w4_scales)
+        load_xr(0, 0, 4)
+        load_words(x4, x4_words)
+        load_scales(x4s, x4_scales)
+        load_xr(1, 0, 4)
+        load_xr(2, 0, 4)
+        load_xr(0, 4, 8)
+        load_xr(1, 4, 8)
+        load_xr(2, 4, 6)
+        load_xr(2, 6, 8)
+
+        for i in range(6):
+            nc.tensor.matmul_mx(
+                out=acc[7][:],
+                lhsT=w4[:, 0, : 2 * P].bitcast(FP4X4),
+                lhsT_scale=w4s[:, 0, :P],
+                rhs=w4[:, 0, :].bitcast(FP4X4),
+                rhs_scale=w4s[:, 0, :],
+                start=True,
+                stop=True,
+            )
+        for a in range(PASSES):
+            v_copy(a, 0, 2)
+            s_copy(a, 2, 4)
+            quant(a, 0, 2)
+            quant(a, 2, 4)
+            if a == 0:
+                for i in range(4):
+                    mm_x4(i)
+        for i in range(4, 8):
+            mm_x4(i)
+
+        relu(0)
+        for i in range(1, 4):
+            relu(i)
+            s_square(i - 1)
+        s_square(3)
+        for i in range(4):
+            store(i)
+
+        v_copy(0, 4, 6)
+        v_copy(0, 6, 8)
+        quant(0, 4, 6)
+        quant(0, 6, 8)
+        v_copy(1, 4, 6)
+        v_copy(1, 6, 7)
+        s_copy(1, 7, 8)
+        v_copy(2, 4, 6)
+        s_copy(2, 6, 7)
+        quant(1, 4, 6)
+        quant(2, 4, 5)
+        quant(2, 5, 6)
+        quant(1, 6, 8)
+        v_copy(2, 7, 8)
+        quant(2, 6, 7)
+        quant(2, 7, 8)
+        relu(4)
+        relu(5)
+        relu(6)
+        v_square(4)
+        store(4)
+        v_square(5)
+        store(5)
+        s_square(6)
+        store(6)
+        nc.vector.tensor_scalar_max(out=rel[7][:], in0=acc[7][:], scalar1=0.0)
+        left, right = slice(0, N // 2), slice(N // 2, N)
+        v_square(7, left)
+        s_square(7, right)
+        store(7, left)
+        store(7, right)

@@ -45,11 +45,11 @@ def tile_mix_xres_tm_relu2_kernel(tc, x4_words, x4_scales, xr, w4_words, w4_scal
         def load_words(tile, words):
             nc.sync.dma_start(out=tile[:].bitcast(I32), in_=words.rearrange("a p n -> p a n").bitcast(I32))
 
-        def load_scales(tile, rows):
-            for q in range(4):
+        def load_scales(tile, rows, r0, r1):
+            for r in range(r0, r1):
                 nc.sync.dma_start(
-                    out=tile[:].bitcast(I32)[32 * q : 32 * q + 4, :, :],
-                    in_=rows[:, 4 * q : 4 * q + 4, :].rearrange("a r n -> r a n").bitcast(I32),
+                    out=tile[:].bitcast(I32)[r:P:32, :, :],
+                    in_=rows[:, r:16:4, :].rearrange("a q n -> q a n").bitcast(I32),
                 )
 
         raw = {}
@@ -81,8 +81,6 @@ def tile_mix_xres_tm_relu2_kernel(tc, x4_words, x4_scales, xr, w4_words, w4_scal
                 scales=scales[a][:, cols],
                 in_=bf[a][:, cols, :].rearrange("p t j -> p (t j)"),
             )
-            for i in range(i0, i1):
-                mm_xr(a, i)
 
         def mm_x4(i):
             for a in range(PASSES):
@@ -92,7 +90,7 @@ def tile_mix_xres_tm_relu2_kernel(tc, x4_words, x4_scales, xr, w4_words, w4_scal
                     lhsT_scale=x4s[:, a, P * i : P * (i + 1)],
                     rhs=w4[:, a, :].bitcast(FP4X4),
                     rhs_scale=w4s[:, a, :],
-                    start=(a == 0 and i >= 4),
+                    start=(a == 0),
                     stop=False,
                 )
 
@@ -103,7 +101,7 @@ def tile_mix_xres_tm_relu2_kernel(tc, x4_words, x4_scales, xr, w4_words, w4_scal
                 lhsT_scale=scales[a][:, P * i : P * (i + 1)],
                 rhs=w4[:, a, :].bitcast(FP4X4),
                 rhs_scale=w4s[:, a, :],
-                start=(a == 0 and i < 4),
+                start=False,
                 stop=(a == PASSES - 1),
             )
 
@@ -121,18 +119,30 @@ def tile_mix_xres_tm_relu2_kernel(tc, x4_words, x4_scales, xr, w4_words, w4_scal
 
         nc.scalar.activation(out=warm[:], in_=warm[:], func=ACT.Relu)
         load_words(w4, w4_words)
-        load_scales(w4s, w4_scales)
-        load_xr(0, 0, 4)
+        load_scales(w4s, w4_scales, 0, 4)
+        load_scales(x4s, x4_scales, 0, 2)
         load_words(x4, x4_words)
-        load_scales(x4s, x4_scales)
-        load_xr(1, 0, 4)
-        load_xr(2, 0, 4)
-        load_xr(0, 4, 8)
-        load_xr(1, 4, 8)
-        load_xr(2, 4, 6)
-        load_xr(2, 6, 8)
+        load_scales(x4s, x4_scales, 2, 4)
+        for c in range(4):
+            for a in range(PASSES):
+                load_xr(a, 2 * c, 2 * c + 2)
 
-        for i in range(6):
+        def step(a, i0, i1):
+            quant(a, i0, i1)
+            for i in range(i0, i1):
+                mm_xr(a, i)
+
+        def s_finish(i0, i1):
+            for i in range(i0, i1):
+                relu(i)
+            for i in range(i0, i1):
+                s_square(i)
+                store(i)
+
+        def v_relu(i, cols=slice(0, N)):
+            nc.vector.tensor_scalar_max(out=rel[i][:, cols], in0=acc[i][:, cols], scalar1=0.0)
+
+        for i in range(4):
             nc.tensor.matmul_mx(
                 out=acc[7][:],
                 lhsT=w4[:, 0, : 2 * P].bitcast(FP4X4),
@@ -142,53 +152,31 @@ def tile_mix_xres_tm_relu2_kernel(tc, x4_words, x4_scales, xr, w4_words, w4_scal
                 start=True,
                 stop=True,
             )
-        for a in range(PASSES):
-            v_copy(a, 0, 2)
-            s_copy(a, 2, 4)
-            quant(a, 0, 2)
-            quant(a, 2, 4)
-            if a == 0:
-                for i in range(4):
-                    mm_x4(i)
-        for i in range(4, 8):
-            mm_x4(i)
 
-        relu(0)
-        for i in range(1, 4):
-            relu(i)
-            s_square(i - 1)
-        s_square(3)
-        for i in range(4):
-            store(i)
-
-        v_copy(0, 4, 6)
-        v_copy(0, 6, 8)
-        quant(0, 4, 6)
-        quant(0, 6, 8)
-        v_copy(1, 4, 6)
-        v_copy(1, 6, 7)
-        s_copy(1, 7, 8)
-        v_copy(2, 4, 6)
-        s_copy(2, 6, 7)
-        quant(1, 4, 6)
-        quant(2, 4, 5)
-        quant(2, 5, 6)
-        quant(1, 6, 8)
-        v_copy(2, 7, 8)
-        quant(2, 6, 7)
-        quant(2, 7, 8)
-        relu(4)
-        relu(5)
-        relu(6)
-        v_square(4)
-        store(4)
-        v_square(5)
-        store(5)
-        s_square(6)
-        store(6)
-        nc.vector.tensor_scalar_max(out=rel[7][:], in0=acc[7][:], scalar1=0.0)
+        mm_x4(0)
+        mm_x4(1)
+        mm_x4(2)
+        for i in range(0, TILES, 2):
+            for a in range(PASSES):
+                v_copy(a, i, i + 1)
+                if i == 0 or a == 0:
+                    s_copy(a, i + 1, i + 2)
+                else:
+                    v_copy(a, i + 1, i + 2)
+                if a == 0 and i > 0:
+                    s_finish(i - 2, i)
+                step(a, i, i + 1)
+                step(a, i + 1, i + 2)
+                if a != 1 and i + 3 + a // 2 < TILES:
+                    mm_x4(i + 3 + a // 2)
         left, right = slice(0, N // 2), slice(N // 2, N)
+        relu(6, left)
+        relu(6, right)
+        s_square(6, left)
+        s_square(6, right)
+        store(6)
+        v_relu(7, left)
+        v_relu(7, right)
         v_square(7, left)
-        s_square(7, right)
-        store(7, left)
-        store(7, right)
+        v_square(7, right)
+        store(7)

@@ -123,9 +123,16 @@ def tile_mix_xres_tm_relu2_kernel(tc, x4_words, x4_scales, xr, w4_words, w4_scal
         load_scales(x4s, x4_scales, 0, 2)
         load_words(x4, x4_words)
         load_scales(x4s, x4_scales, 2, 4)
-        for c in range(4):
-            for a in range(PASSES):
-                load_xr(a, 2 * c, 2 * c + 2)
+        load_xr(0, 0, 4)
+        load_xr(1, 0, 4)
+        load_xr(2, 0, 2)
+        load_xr(2, 2, 4)
+        load_xr(0, 4, 8)
+        load_xr(1, 4, 6)
+        load_xr(2, 4, 6)
+        load_xr(1, 6, 8)
+        load_xr(2, 6, 7)
+        load_xr(2, 7, 8)
 
         def step(a, i0, i1):
             quant(a, i0, i1)
@@ -153,22 +160,67 @@ def tile_mix_xres_tm_relu2_kernel(tc, x4_words, x4_scales, xr, w4_words, w4_scal
                 stop=True,
             )
 
-        mm_x4(0)
-        mm_x4(1)
-        mm_x4(2)
-        for i in range(0, TILES, 2):
-            for a in range(PASSES):
-                v_copy(a, i, i + 1)
-                if i == 0 or a == 0:
-                    s_copy(a, i + 1, i + 2)
-                else:
-                    v_copy(a, i + 1, i + 2)
-                if a == 0 and i > 0:
-                    s_finish(i - 2, i)
-                step(a, i, i + 1)
-                step(a, i + 1, i + 2)
-                if a != 1 and i + 3 + a // 2 < TILES:
-                    mm_x4(i + 3 + a // 2)
+        for i in range(5):
+            mm_x4(i)
+        v_copy(0, 0, 2)
+        s_copy(0, 2, 4)
+        step(0, 0, 2)
+        step(0, 2, 4)
+        mm_x4(5)
+        v_copy(1, 0, 1)
+        v_copy(1, 1, 2)
+        s_copy(1, 2, 4)
+        step(1, 0, 1)
+        step(1, 1, 2)
+        v_copy(2, 0, 1)
+        s_copy(2, 1, 2)
+        quant(1, 2, 4)
+        step(2, 0, 1)
+        step(2, 1, 2)
+        mm_xr(1, 2)
+        mm_xr(1, 3)
+        v_copy(2, 2, 3)
+        v_copy(2, 3, 4)
+        step(2, 2, 3)
+        step(2, 3, 4)
+        mm_x4(6)
+        mm_x4(7)
+        s_finish(0, 2)
+        v_relu(2)
+        v_copy(0, 4, 6)
+        s_copy(0, 7, 8)
+        v_copy(0, 6, 7)
+        step(0, 4, 6)
+        relu(3)
+        s_square(2)
+        store(2)
+        s_square(3)
+        store(3)
+        v_copy(1, 4, 5)
+        v_copy(1, 5, 6)
+        step(1, 4, 5)
+        step(1, 5, 6)
+        v_copy(2, 4, 5)
+        s_copy(2, 5, 6)
+        quant(0, 6, 8)
+        step(2, 4, 5)
+        step(2, 5, 6)
+        mm_xr(0, 6)
+        mm_xr(0, 7)
+        v_copy(1, 6, 7)
+        s_copy(1, 7, 8)
+        relu(4)
+        relu(5)
+        s_square(4)
+        store(4)
+        v_copy(2, 6, 7)
+        step(1, 6, 7)
+        step(2, 6, 7)
+        step(1, 7, 8)
+        v_copy(2, 7, 8)
+        step(2, 7, 8)
+        v_square(5)
+        store(5)
         left, right = slice(0, N // 2), slice(N // 2, N)
         relu(6, left)
         relu(6, right)
@@ -178,5 +230,6 @@ def tile_mix_xres_tm_relu2_kernel(tc, x4_words, x4_scales, xr, w4_words, w4_scal
         v_relu(7, left)
         v_relu(7, right)
         v_square(7, left)
+        store(7, left)
         v_square(7, right)
-        store(7)
+        store(7, right)

@@ -15,8 +15,17 @@ FP4X4 = mybir.dt.float4_e2m1fn_x4
 ACT = mybir.ActivationFunctionType
 
 P = 128
-PASSES = K // 512
+PACK = 4
+K_PASS = P * PACK
+PASSES = K // K_PASS
 TILES = T // P
+QUADRANT = 32
+WARM_UP_PASSES = 4
+
+XR_LOADS = (
+    (0, 0, 4), (1, 0, 4), (2, 0, 2), (2, 2, 4),
+    (0, 4, 8), (1, 4, 6), (2, 4, 6), (1, 6, 8), (2, 6, 7), (2, 7, 8),
+)
 
 
 def tile_mix_xres_tm_relu2_kernel(tc, x4_words, x4_scales, xr, w4_words, w4_scales, out):
@@ -27,209 +36,184 @@ def tile_mix_xres_tm_relu2_kernel(tc, x4_words, x4_scales, xr, w4_words, w4_scal
         ctx.enter_context(tc.manual_schedule())
 
         w4 = keep.tile([P, PASSES, 2 * N], U8, name="w4", align_bytes=64)
-        w4s = keep.tile([P, PASSES, N], U8, name="w4s", align_bytes=64)
+        w4_plane = keep.tile([P, PASSES, N], U8, name="w4_plane", align_bytes=64)
         x4 = keep.tile([P, PASSES, 2 * T], U8, name="x4", align_bytes=64)
-        x4s = keep.tile([P, PASSES, T], U8, name="x4s", align_bytes=64)
-        bf = [keep.tile([P, T, 4], BF16, name=f"bf{a}", align_bytes=64) for a in range(PASSES)]
+        x4_plane = keep.tile([P, PASSES, T], U8, name="x4_plane", align_bytes=64)
+        rounded = [keep.tile([P, T, PACK], BF16, name=f"rounded{a}", align_bytes=64) for a in range(PASSES)]
         codes = [keep.tile([P, T], U32, name=f"codes{a}", align_bytes=64) for a in range(PASSES)]
-        scales = [keep.tile([P, T], U8, name=f"scales{a}", align_bytes=64) for a in range(PASSES)]
-        rel = [keep.tile([P, N], F32, name=f"rel{i}", align_bytes=64) for i in range(TILES)]
-        res = [keep.tile([P, N], F32, name=f"res{i}", align_bytes=64) for i in range(TILES)]
-        warm = keep.tile([P, 1], F32, name="warm")
+        xr_plane = [keep.tile([P, T], U8, name=f"xr_plane{a}", align_bytes=64) for a in range(PASSES)]
+        positive = [keep.tile([P, N], F32, name=f"positive{i}", align_bytes=64) for i in range(TILES)]
+        result = [keep.tile([P, N], F32, name=f"result{i}", align_bytes=64) for i in range(TILES)]
+        table_probe = keep.tile([P, 1], F32, name="table_probe")
         acc = [psum.tile([P, N], F32, name=f"acc{i}") for i in range(TILES)]
 
-        nc.vector.memset(w4s[:].rearrange("p a n -> p (a n)").bitcast(I32), 0)
-        nc.vector.memset(x4s[:].rearrange("p a n -> p (a n)").bitcast(I32), 0)
-        nc.gpsimd.memset(warm[:], 0.0)
+        nc.vector.memset(w4_plane[:].rearrange("p a n -> p (a n)").bitcast(I32), 0)
+        nc.vector.memset(x4_plane[:].rearrange("p a n -> p (a n)").bitcast(I32), 0)
+        nc.gpsimd.memset(table_probe[:], 0.0)
 
         def load_words(tile, words):
             nc.sync.dma_start(out=tile[:].bitcast(I32), in_=words.rearrange("a p n -> p a n").bitcast(I32))
 
-        def load_scales(tile, rows, r0, r1):
-            for r in range(r0, r1):
+        def load_scales(plane, scales, rows):
+            for r in rows:
                 nc.sync.dma_start(
-                    out=tile[:].bitcast(I32)[r:P:32, :, :],
-                    in_=rows[:, r:16:4, :].rearrange("a q n -> q a n").bitcast(I32),
+                    out=plane[:].bitcast(I32)[r:P:QUADRANT, :, :],
+                    in_=scales[:, r:16:4, :].rearrange("a g n -> g a n").bitcast(I32),
                 )
 
-        raw = {}
+        landed = {}
 
-        def load_xr(a, i0, i1):
-            tile = keep.tile([P, 4, P * (i1 - i0)], F32, name=f"raw{a}_{i0}", align_bytes=64)
-            rows = xr[512 * a : 512 * (a + 1), P * i0 : P * i1]
-            nc.sync.dma_start(out=tile[:], in_=rows.rearrange("(p j) t -> p j t", j=4))
-            for i in range(i0, i1):
-                raw[a, i] = (tile, P * (i - i0))
+        def load_xr(a, first, end):
+            raw = keep.tile([P, PACK, P * (end - first)], F32, name=f"raw{a}_{first}", align_bytes=64)
+            rows = xr[K_PASS * a : K_PASS * (a + 1), P * first : P * end]
+            nc.sync.dma_start(out=raw[:], in_=rows.rearrange("(p j) t -> p j t", j=PACK))
+            for i in range(first, end):
+                landed[a, i] = (raw, P * (i - first))
 
-        def copy(engine_copy, a, i0, i1):
-            tile, t0 = raw[a, i0]
-            engine_copy(
-                out=bf[a][:, P * i0 : P * i1, :].rearrange("p (c i) j -> p c j i", i=4),
-                in_=tile[:, :, t0 : t0 + P * (i1 - i0)].rearrange("p j (c i) -> p c j i", i=4),
+        def interleave(copy, a, first, end):
+            raw, t0 = landed[a, first]
+            copy(
+                out=rounded[a][:, P * first : P * end, :].rearrange("p (c i) j -> p c j i", i=4),
+                in_=raw[:, :, t0 : t0 + P * (end - first)].rearrange("p j (c i) -> p c j i", i=4),
             )
 
-        def v_copy(a, i0, i1):
-            copy(nc.vector.tensor_copy, a, i0, i1)
-
-        def s_copy(a, i0, i1):
-            copy(nc.scalar.copy, a, i0, i1)
-
-        def quant(a, i0, i1):
-            cols = slice(P * i0, P * i1)
+        def quantize(a, first, end):
+            cols = slice(P * first, P * end)
             nc.vector.quantize_mx(
                 out=codes[a][:, cols].bitcast(FP8X4),
-                scales=scales[a][:, cols],
-                in_=bf[a][:, cols, :].rearrange("p t j -> p (t j)"),
+                scales=xr_plane[a][:, cols],
+                in_=rounded[a][:, cols, :].rearrange("p t j -> p (t j)"),
             )
 
-        def mm_x4(i):
-            for a in range(PASSES):
-                nc.tensor.matmul_mx(
-                    out=acc[i][:],
-                    lhsT=x4[:, a, 2 * P * i : 2 * P * (i + 1)].bitcast(FP4X4),
-                    lhsT_scale=x4s[:, a, P * i : P * (i + 1)],
-                    rhs=w4[:, a, :].bitcast(FP4X4),
-                    rhs_scale=w4s[:, a, :],
-                    start=(a == 0),
-                    stop=False,
-                )
-
-        def mm_xr(a, i):
+        def mx_pass(bank, a, lhsT, lhsT_scale, start, stop):
             nc.tensor.matmul_mx(
-                out=acc[i][:],
-                lhsT=codes[a][:, P * i : P * (i + 1)].bitcast(FP8X4),
-                lhsT_scale=scales[a][:, P * i : P * (i + 1)],
+                out=bank[:],
+                lhsT=lhsT,
+                lhsT_scale=lhsT_scale,
                 rhs=w4[:, a, :].bitcast(FP4X4),
-                rhs_scale=w4s[:, a, :],
-                start=False,
-                stop=(a == PASSES - 1),
+                rhs_scale=w4_plane[:, a, :],
+                start=start,
+                stop=stop,
             )
 
-        def relu(i, cols=slice(0, N)):
-            nc.scalar.activation(out=rel[i][:, cols], in_=acc[i][:, cols], func=ACT.Relu)
+        def x4_passes(i):
+            for a in range(PASSES):
+                words = x4[:, a, 2 * P * i : 2 * P * (i + 1)].bitcast(FP4X4)
+                mx_pass(acc[i], a, words, x4_plane[:, a, P * i : P * (i + 1)], start=(a == 0), stop=False)
 
-        def v_square(i, cols=slice(0, N)):
-            nc.vector.tensor_mul(out=res[i][:, cols], in0=rel[i][:, cols], in1=rel[i][:, cols])
+        def xr_passes(a, first, end):
+            for i in range(first, end):
+                cols = slice(P * i, P * (i + 1))
+                words = codes[a][:, cols].bitcast(FP8X4)
+                mx_pass(acc[i], a, words, xr_plane[a][:, cols], start=False, stop=(a == PASSES - 1))
 
-        def s_square(i, cols=slice(0, N)):
-            nc.scalar.activation(out=res[i][:, cols], in_=rel[i][:, cols], func=ACT.Square)
+        def quantize_and_multiply(a, first, end):
+            quantize(a, first, end)
+            xr_passes(a, first, end)
 
-        def store(i, cols=slice(0, N)):
-            nc.sync.dma_start(out=out[P * i : P * (i + 1), cols], in_=res[i][:, cols])
+        whole = slice(0, N)
+        halves = (slice(0, N // 2), slice(N // 2, N))
 
-        nc.scalar.activation(out=warm[:], in_=warm[:], func=ACT.Relu)
-        load_words(w4, w4_words)
-        load_scales(w4s, w4_scales, 0, 4)
-        load_scales(x4s, x4_scales, 0, 2)
-        load_words(x4, x4_words)
-        load_scales(x4s, x4_scales, 2, 4)
-        load_xr(0, 0, 4)
-        load_xr(1, 0, 4)
-        load_xr(2, 0, 2)
-        load_xr(2, 2, 4)
-        load_xr(0, 4, 8)
-        load_xr(1, 4, 6)
-        load_xr(2, 4, 6)
-        load_xr(1, 6, 8)
-        load_xr(2, 6, 7)
-        load_xr(2, 7, 8)
+        def scalar_relu(i, cols=whole):
+            nc.scalar.activation(out=positive[i][:, cols], in_=acc[i][:, cols], func=ACT.Relu)
 
-        def step(a, i0, i1):
-            quant(a, i0, i1)
-            for i in range(i0, i1):
-                mm_xr(a, i)
+        def scalar_square(i, cols=whole):
+            nc.scalar.activation(out=result[i][:, cols], in_=positive[i][:, cols], func=ACT.Square)
 
-        def s_finish(i0, i1):
-            for i in range(i0, i1):
-                relu(i)
-            for i in range(i0, i1):
-                s_square(i)
+        def vector_relu(i, cols=whole):
+            nc.vector.tensor_scalar_max(out=positive[i][:, cols], in0=acc[i][:, cols], scalar1=0.0)
+
+        def vector_square(i, cols=whole):
+            nc.vector.tensor_mul(out=result[i][:, cols], in0=positive[i][:, cols], in1=positive[i][:, cols])
+
+        def scalar_finish(first, end):
+            for i in range(first, end):
+                scalar_relu(i)
+            for i in range(first, end):
+                scalar_square(i)
                 store(i)
 
-        def v_relu(i, cols=slice(0, N)):
-            nc.vector.tensor_scalar_max(out=rel[i][:, cols], in0=acc[i][:, cols], scalar1=0.0)
+        def store(i, cols=whole):
+            nc.sync.dma_start(out=out[P * i : P * (i + 1), cols], in_=result[i][:, cols])
 
-        for i in range(4):
-            nc.tensor.matmul_mx(
-                out=acc[7][:],
-                lhsT=w4[:, 0, : 2 * P].bitcast(FP4X4),
-                lhsT_scale=w4s[:, 0, :P],
-                rhs=w4[:, 0, :].bitcast(FP4X4),
-                rhs_scale=w4s[:, 0, :],
-                start=True,
-                stop=True,
-            )
+        on_vector, on_scalar = nc.vector.tensor_copy, nc.scalar.copy
+
+        nc.scalar.activation(out=table_probe[:], in_=table_probe[:], func=ACT.Relu)
+
+        load_words(w4, w4_words)
+        load_scales(w4_plane, w4_scales, range(4))
+        load_scales(x4_plane, x4_scales, range(2))
+        load_words(x4, x4_words)
+        load_scales(x4_plane, x4_scales, range(2, 4))
+        for a, first, end in XR_LOADS:
+            load_xr(a, first, end)
+
+        for repeat in range(WARM_UP_PASSES):
+            mx_pass(acc[TILES - 1], 0, w4[:, 0, : 2 * P].bitcast(FP4X4), w4_plane[:, 0, :P], start=True, stop=True)
 
         for i in range(5):
-            mm_x4(i)
-        v_copy(0, 0, 2)
-        s_copy(0, 2, 4)
-        step(0, 0, 2)
-        step(0, 2, 4)
-        mm_x4(5)
-        v_copy(1, 0, 1)
-        v_copy(1, 1, 2)
-        s_copy(1, 2, 4)
-        step(1, 0, 1)
-        step(1, 1, 2)
-        v_copy(2, 0, 1)
-        s_copy(2, 1, 2)
-        quant(1, 2, 4)
-        step(2, 0, 1)
-        step(2, 1, 2)
-        mm_xr(1, 2)
-        mm_xr(1, 3)
-        v_copy(2, 2, 3)
-        v_copy(2, 3, 4)
-        step(2, 2, 3)
-        step(2, 3, 4)
-        mm_x4(6)
-        mm_x4(7)
-        s_finish(0, 2)
-        v_relu(2)
-        v_copy(0, 4, 6)
-        s_copy(0, 7, 8)
-        v_copy(0, 6, 7)
-        step(0, 4, 6)
-        relu(3)
-        s_square(2)
-        store(2)
-        s_square(3)
-        store(3)
-        v_copy(1, 4, 5)
-        v_copy(1, 5, 6)
-        step(1, 4, 5)
-        step(1, 5, 6)
-        v_copy(2, 4, 5)
-        s_copy(2, 5, 6)
-        quant(0, 6, 8)
-        step(2, 4, 5)
-        step(2, 5, 6)
-        mm_xr(0, 6)
-        mm_xr(0, 7)
-        v_copy(1, 6, 7)
-        s_copy(1, 7, 8)
-        relu(4)
-        relu(5)
-        s_square(4)
+            x4_passes(i)
+        interleave(on_vector, 0, 0, 2)
+        interleave(on_scalar, 0, 2, 4)
+        quantize_and_multiply(0, 0, 2)
+        quantize_and_multiply(0, 2, 4)
+        x4_passes(5)
+        interleave(on_vector, 1, 0, 1)
+        interleave(on_vector, 1, 1, 2)
+        interleave(on_scalar, 1, 2, 4)
+        quantize_and_multiply(1, 0, 1)
+        quantize_and_multiply(1, 1, 2)
+        interleave(on_vector, 2, 0, 1)
+        interleave(on_scalar, 2, 1, 2)
+        quantize(1, 2, 4)
+        quantize_and_multiply(2, 0, 1)
+        quantize_and_multiply(2, 1, 2)
+        xr_passes(1, 2, 4)
+        interleave(on_vector, 2, 2, 3)
+        interleave(on_vector, 2, 3, 4)
+        quantize_and_multiply(2, 2, 3)
+        quantize_and_multiply(2, 3, 4)
+        x4_passes(6)
+        x4_passes(7)
+
+        scalar_finish(0, 2)
+        interleave(on_vector, 0, 4, 6)
+        interleave(on_vector, 0, 6, 8)
+        quantize_and_multiply(0, 4, 6)
+        scalar_finish(2, 4)
+        interleave(on_vector, 1, 4, 5)
+        interleave(on_vector, 1, 5, 6)
+        quantize_and_multiply(1, 4, 5)
+        quantize_and_multiply(1, 5, 6)
+        interleave(on_vector, 2, 4, 5)
+        interleave(on_scalar, 2, 5, 6)
+        quantize(0, 6, 8)
+        quantize_and_multiply(2, 4, 5)
+        quantize_and_multiply(2, 5, 6)
+        xr_passes(0, 6, 8)
+        interleave(on_vector, 1, 6, 7)
+        interleave(on_scalar, 1, 7, 8)
+        scalar_relu(4)
+        scalar_relu(5)
+        scalar_square(4)
         store(4)
-        v_copy(2, 6, 7)
-        step(1, 6, 7)
-        step(2, 6, 7)
-        step(1, 7, 8)
-        v_copy(2, 7, 8)
-        step(2, 7, 8)
-        v_square(5)
+
+        interleave(on_vector, 2, 6, 7)
+        quantize_and_multiply(1, 6, 7)
+        quantize_and_multiply(2, 6, 7)
+        interleave(on_vector, 2, 7, 8)
+        quantize_and_multiply(1, 7, 8)
+        quantize_and_multiply(2, 7, 8)
+
+        vector_square(5)
         store(5)
-        left, right = slice(0, N // 2), slice(N // 2, N)
-        relu(6, left)
-        relu(6, right)
-        s_square(6, left)
-        s_square(6, right)
+        for cols in halves:
+            scalar_relu(6, cols)
+        for cols in halves:
+            scalar_square(6, cols)
         store(6)
-        v_relu(7, left)
-        v_relu(7, right)
-        v_square(7, left)
-        store(7, left)
-        v_square(7, right)
-        store(7, right)
+        for cols in halves:
+            vector_relu(7, cols)
+        for square, cols in zip((scalar_square, vector_square), halves):
+            square(7, cols)
+            store(7, cols)

@@ -23,8 +23,8 @@ QUADRANT = 32
 WARM_UP_PASSES = 4
 
 XR_LOADS = (
-    (0, 0, 4), (1, 0, 4), (2, 0, 2), (2, 2, 4),
-    (0, 4, 8), (1, 4, 6), (2, 4, 6), (1, 6, 8), (2, 6, 7), (2, 7, 8),
+    (0, 0, 8), (1, 0, 4), (2, 0, 2), (2, 2, 4),
+    (1, 4, 6), (2, 4, 6), (1, 6, 8), (2, 6, 7), (2, 7, 8),
 )
 
 
@@ -51,8 +51,11 @@ def tile_mix_xres_tm_relu2_kernel(tc, x4_words, x4_scales, xr, w4_words, w4_scal
         nc.vector.memset(x4_plane[:].rearrange("p a n -> p (a n)").bitcast(I32), 0)
         nc.gpsimd.memset(table_probe[:], 0.0)
 
-        def load_words(tile, words):
-            nc.sync.dma_start(out=tile[:].bitcast(I32), in_=words.rearrange("a p n -> p a n").bitcast(I32))
+        def load_words(tile, words, first, end):
+            nc.sync.dma_start(
+                out=tile[:, first:end, :].bitcast(I32),
+                in_=words[first:end].rearrange("a p n -> p a n").bitcast(I32),
+            )
 
         def load_scales(plane, scales, rows):
             for r in rows:
@@ -96,8 +99,8 @@ def tile_mix_xres_tm_relu2_kernel(tc, x4_words, x4_scales, xr, w4_words, w4_scal
                 stop=stop,
             )
 
-        def x4_passes(i):
-            for a in range(PASSES):
+        def x4_passes(a, first, end):
+            for i in range(first, end):
                 words = x4[:, a, 2 * P * i : 2 * P * (i + 1)].bitcast(FP4X4)
                 mx_pass(acc[i], a, words, x4_plane[:, a, P * i : P * (i + 1)], start=(a == 0), stop=False)
 
@@ -140,71 +143,74 @@ def tile_mix_xres_tm_relu2_kernel(tc, x4_words, x4_scales, xr, w4_words, w4_scal
 
         nc.scalar.activation(out=table_probe[:], in_=table_probe[:], func=ACT.Relu)
 
-        load_words(w4, w4_words)
+        load_words(w4, w4_words, 0, 3)
         load_scales(w4_plane, w4_scales, range(4))
         load_scales(x4_plane, x4_scales, range(2))
-        load_words(x4, x4_words)
+        load_words(x4, x4_words, 0, 3)
         load_scales(x4_plane, x4_scales, range(2, 4))
         for a, first, end in XR_LOADS:
             load_xr(a, first, end)
 
         for repeat in range(WARM_UP_PASSES):
             mx_pass(acc[TILES - 1], 0, w4[:, 0, : 2 * P].bitcast(FP4X4), w4_plane[:, 0, :P], start=True, stop=True)
-
-        for i in range(5):
-            x4_passes(i)
+        for a in range(PASSES):
+            x4_passes(a, 0, 4)
+        x4_passes(0, 4, 8)
+        x4_passes(1, 4, 6)
         interleave(on_vector, 0, 0, 2)
-        interleave(on_scalar, 0, 2, 4)
+        interleave(on_scalar, 0, 4, 6)
+        interleave(on_vector, 0, 2, 4)
         quantize_and_multiply(0, 0, 2)
         quantize_and_multiply(0, 2, 4)
-        x4_passes(5)
+        interleave(on_scalar, 0, 6, 8)
+        quantize_and_multiply(0, 4, 6)
         interleave(on_vector, 1, 0, 1)
         interleave(on_vector, 1, 1, 2)
         interleave(on_scalar, 1, 2, 4)
         quantize_and_multiply(1, 0, 1)
         quantize_and_multiply(1, 1, 2)
+        quantize(0, 6, 8)
         interleave(on_vector, 2, 0, 1)
         interleave(on_scalar, 2, 1, 2)
-        quantize(1, 2, 4)
+        quantize_and_multiply(1, 2, 4)
         quantize_and_multiply(2, 0, 1)
         quantize_and_multiply(2, 1, 2)
-        xr_passes(1, 2, 4)
+        x4_passes(2, 4, 6)
         interleave(on_vector, 2, 2, 3)
         interleave(on_vector, 2, 3, 4)
         quantize_and_multiply(2, 2, 3)
         quantize_and_multiply(2, 3, 4)
-        x4_passes(6)
-        x4_passes(7)
-
+        xr_passes(0, 6, 8)
+        x4_passes(1, 6, 8)
         scalar_finish(0, 2)
-        interleave(on_vector, 0, 4, 6)
-        interleave(on_vector, 0, 6, 8)
-        quantize_and_multiply(0, 4, 6)
-        scalar_finish(2, 4)
         interleave(on_vector, 1, 4, 5)
         interleave(on_vector, 1, 5, 6)
         quantize_and_multiply(1, 4, 5)
         quantize_and_multiply(1, 5, 6)
+        x4_passes(2, 6, 8)
+        vector_relu(3)
+        scalar_relu(2)
+        scalar_square(3)
+        scalar_square(2)
+        store(2)
+        store(3)
         interleave(on_vector, 2, 4, 5)
-        interleave(on_scalar, 2, 5, 6)
-        quantize(0, 6, 8)
+        interleave(on_vector, 2, 5, 6)
         quantize_and_multiply(2, 4, 5)
         quantize_and_multiply(2, 5, 6)
-        xr_passes(0, 6, 8)
         interleave(on_vector, 1, 6, 7)
-        interleave(on_scalar, 1, 7, 8)
+        interleave(on_vector, 1, 7, 8)
         scalar_relu(4)
         scalar_relu(5)
         scalar_square(4)
         store(4)
-
-        interleave(on_vector, 2, 6, 7)
         quantize_and_multiply(1, 6, 7)
+        interleave(on_vector, 2, 6, 7)
+        quantize(1, 7, 8)
         quantize_and_multiply(2, 6, 7)
+        xr_passes(1, 7, 8)
         interleave(on_vector, 2, 7, 8)
-        quantize_and_multiply(1, 7, 8)
         quantize_and_multiply(2, 7, 8)
-
         vector_square(5)
         store(5)
         for cols in halves:

@@ -20,7 +20,7 @@ K_PASS = P * PACK
 PASSES = K // K_PASS
 TILES = T // P
 QUADRANT = 32
-WARM_UP_PASSES = 4
+WARM_UP_PASSES = 3
 
 XR_LOADS = (
     (0, 0, 8), (1, 0, 4), (2, 0, 2), (2, 2, 4),
@@ -143,51 +143,52 @@ def tile_mix_xres_tm_relu2_kernel(tc, x4_words, x4_scales, xr, w4_words, w4_scal
 
         nc.scalar.activation(out=table_probe[:], in_=table_probe[:], func=ACT.Relu)
 
-        load_words(w4, w4_words, 0, 3)
-        load_scales(w4_plane, w4_scales, range(4))
-        load_scales(x4_plane, x4_scales, range(2))
-        load_words(x4, x4_words, 0, 3)
+        load_words(w4, w4_words, 0, 1)
+        load_scales(w4_plane, w4_scales, range(0, 4))
+        load_scales(x4_plane, x4_scales, range(0, 2))
+        load_words(x4, x4_words, 0, 2)
         load_scales(x4_plane, x4_scales, range(2, 4))
+        load_words(w4, w4_words, 1, 3)
+        load_words(x4, x4_words, 2, 3)
         for a, first, end in XR_LOADS:
             load_xr(a, first, end)
 
         for repeat in range(WARM_UP_PASSES):
             mx_pass(acc[TILES - 1], 0, w4[:, 0, : 2 * P].bitcast(FP4X4), w4_plane[:, 0, :P], start=True, stop=True)
-        for a in range(PASSES):
-            x4_passes(a, 0, 4)
-        x4_passes(0, 4, 8)
-        x4_passes(1, 4, 6)
+        x4_passes(0, 0, 8)
+        x4_passes(1, 0, 8)
+        x4_passes(2, 0, 6)
         interleave(on_vector, 0, 0, 2)
         interleave(on_scalar, 0, 4, 6)
         interleave(on_vector, 0, 2, 4)
         quantize_and_multiply(0, 0, 2)
         quantize_and_multiply(0, 2, 4)
         interleave(on_scalar, 0, 6, 8)
-        quantize_and_multiply(0, 4, 6)
+        quantize(0, 4, 6)
         interleave(on_vector, 1, 0, 1)
         interleave(on_vector, 1, 1, 2)
         interleave(on_scalar, 1, 2, 4)
         quantize_and_multiply(1, 0, 1)
         quantize_and_multiply(1, 1, 2)
+        xr_passes(0, 4, 6)
         quantize(0, 6, 8)
         interleave(on_vector, 2, 0, 1)
         interleave(on_scalar, 2, 1, 2)
-        quantize_and_multiply(1, 2, 4)
+        quantize(1, 2, 4)
         quantize_and_multiply(2, 0, 1)
         quantize_and_multiply(2, 1, 2)
-        x4_passes(2, 4, 6)
+        xr_passes(1, 2, 4)
         interleave(on_vector, 2, 2, 3)
         interleave(on_vector, 2, 3, 4)
         quantize_and_multiply(2, 2, 3)
         quantize_and_multiply(2, 3, 4)
         xr_passes(0, 6, 8)
-        x4_passes(1, 6, 8)
+        x4_passes(2, 6, 8)
         scalar_finish(0, 2)
         interleave(on_vector, 1, 4, 5)
         interleave(on_vector, 1, 5, 6)
         quantize_and_multiply(1, 4, 5)
         quantize_and_multiply(1, 5, 6)
-        x4_passes(2, 6, 8)
         vector_relu(3)
         scalar_relu(2)
         scalar_square(3)
@@ -204,12 +205,11 @@ def tile_mix_xres_tm_relu2_kernel(tc, x4_words, x4_scales, xr, w4_words, w4_scal
         scalar_relu(5)
         scalar_square(4)
         store(4)
-        quantize_and_multiply(1, 6, 7)
         interleave(on_vector, 2, 6, 7)
-        quantize(1, 7, 8)
+        quantize_and_multiply(1, 6, 7)
         quantize_and_multiply(2, 6, 7)
-        xr_passes(1, 7, 8)
         interleave(on_vector, 2, 7, 8)
+        quantize_and_multiply(1, 7, 8)
         quantize_and_multiply(2, 7, 8)
         vector_square(5)
         store(5)

@@ -20,7 +20,7 @@ K_PASS = P * PACK
 PASSES = K // K_PASS
 TILES = T // P
 QUADRANT = 32
-WARM_UP_PASSES = 3
+WARM_UP_PASSES = 4
 
 XR_LOADS = (
     (0, 0, 8), (1, 0, 4), (2, 0, 2), (2, 2, 4),
@@ -143,12 +143,11 @@ def tile_mix_xres_tm_relu2_kernel(tc, x4_words, x4_scales, xr, w4_words, w4_scal
 
         nc.scalar.activation(out=table_probe[:], in_=table_probe[:], func=ACT.Relu)
 
-        load_words(w4, w4_words, 0, 1)
+        load_words(w4, w4_words, 0, 3)
         load_scales(w4_plane, w4_scales, range(0, 4))
         load_scales(x4_plane, x4_scales, range(0, 2))
         load_words(x4, x4_words, 0, 2)
         load_scales(x4_plane, x4_scales, range(2, 4))
-        load_words(w4, w4_words, 1, 3)
         load_words(x4, x4_words, 2, 3)
         for a, first, end in XR_LOADS:
             load_xr(a, first, end)
@@ -170,56 +169,53 @@ def tile_mix_xres_tm_relu2_kernel(tc, x4_words, x4_scales, xr, w4_words, w4_scal
         interleave(on_scalar, 1, 2, 4)
         quantize_and_multiply(1, 0, 1)
         quantize_and_multiply(1, 1, 2)
-        xr_passes(0, 4, 6)
-        quantize(0, 6, 8)
+        xr_passes(0, 4, 5)
         interleave(on_vector, 2, 0, 1)
         interleave(on_scalar, 2, 1, 2)
         quantize(1, 2, 4)
         quantize_and_multiply(2, 0, 1)
         quantize_and_multiply(2, 1, 2)
         xr_passes(1, 2, 4)
+        quantize(0, 6, 8)
         interleave(on_vector, 2, 2, 3)
         interleave(on_vector, 2, 3, 4)
         quantize_and_multiply(2, 2, 3)
         quantize_and_multiply(2, 3, 4)
-        xr_passes(0, 6, 8)
+        xr_passes(0, 5, 8)
         x4_passes(2, 6, 8)
         scalar_finish(0, 2)
-        interleave(on_vector, 1, 4, 5)
-        interleave(on_vector, 1, 5, 6)
-        quantize_and_multiply(1, 4, 5)
-        quantize_and_multiply(1, 5, 6)
-        vector_relu(3)
-        scalar_relu(2)
-        scalar_square(3)
+        interleave(on_vector, 1, 4, 6)
+        vector_relu(2)
+        quantize_and_multiply(1, 4, 6)
+        scalar_relu(3)
         scalar_square(2)
         store(2)
+        scalar_square(3)
         store(3)
         interleave(on_vector, 2, 4, 5)
         interleave(on_vector, 2, 5, 6)
         quantize_and_multiply(2, 4, 5)
         quantize_and_multiply(2, 5, 6)
-        interleave(on_vector, 1, 6, 7)
-        interleave(on_vector, 1, 7, 8)
-        scalar_relu(4)
-        scalar_relu(5)
-        scalar_square(4)
-        store(4)
+        interleave(on_vector, 1, 6, 8)
         interleave(on_vector, 2, 6, 7)
         quantize_and_multiply(1, 6, 7)
         quantize_and_multiply(2, 6, 7)
         interleave(on_vector, 2, 7, 8)
         quantize_and_multiply(1, 7, 8)
         quantize_and_multiply(2, 7, 8)
-        vector_square(5)
+        scalar_relu(4)
+        scalar_relu(5)
+        scalar_square(4)
+        store(4)
+        scalar_square(5)
         store(5)
         for cols in halves:
-            scalar_relu(6, cols)
+            vector_relu(6, cols)
+        for cols in halves:
+            vector_relu(7, cols)
         for cols in halves:
             scalar_square(6, cols)
         store(6)
-        for cols in halves:
-            vector_relu(7, cols)
-        for square, cols in zip((scalar_square, vector_square), halves):
+        for square, cols in zip((vector_square, scalar_square), halves):
             square(7, cols)
-            store(7, cols)
+        store(7)

@@ -35,15 +35,15 @@ def tile_mix_xres_tm_relu2_kernel(tc, x4_words, x4_scales, xr, w4_words, w4_scal
         psum = ctx.enter_context(tc.psum_pool(name="psum", bufs=1))
         ctx.enter_context(tc.manual_schedule())
 
-        w4 = keep.tile([P, PASSES, 2 * N], U8, name="w4", align_bytes=64)
-        w4_plane = keep.tile([P, PASSES, N], U8, name="w4_plane", align_bytes=64)
-        x4 = keep.tile([P, PASSES, 2 * T], U8, name="x4", align_bytes=64)
-        x4_plane = keep.tile([P, PASSES, T], U8, name="x4_plane", align_bytes=64)
-        rounded = [keep.tile([P, T, PACK], BF16, name=f"rounded{a}", align_bytes=64) for a in range(PASSES)]
-        codes = [keep.tile([P, T], U32, name=f"codes{a}", align_bytes=64) for a in range(PASSES)]
-        xr_plane = [keep.tile([P, T], U8, name=f"xr_plane{a}", align_bytes=64) for a in range(PASSES)]
-        positive = [keep.tile([P, N], F32, name=f"positive{i}", align_bytes=64) for i in range(TILES)]
-        result = [keep.tile([P, N], F32, name=f"result{i}", align_bytes=64) for i in range(TILES)]
+        w4 = keep.tile([P, PASSES, 2 * N], U8, name="w4", align_bytes=256)
+        w4_plane = keep.tile([P, PASSES, N], U8, name="w4_plane", align_bytes=256)
+        x4 = keep.tile([P, PASSES, 2 * T], U8, name="x4", align_bytes=256)
+        x4_plane = keep.tile([P, PASSES, T], U8, name="x4_plane", align_bytes=256)
+        rounded = [keep.tile([P, T, PACK], BF16, name=f"rounded{a}", align_bytes=256) for a in range(PASSES)]
+        codes = [keep.tile([P, T], U32, name=f"codes{a}", align_bytes=256) for a in range(PASSES)]
+        xr_plane = [keep.tile([P, T], U8, name=f"xr_plane{a}", align_bytes=256) for a in range(PASSES)]
+        positive = [keep.tile([P, N], F32, name=f"positive{i}", align_bytes=256) for i in range(TILES)]
+        result = [keep.tile([P, N], F32, name=f"result{i}", align_bytes=256) for i in range(TILES)]
         table_probe = keep.tile([P, 1], F32, name="table_probe")
         acc = [psum.tile([P, N], F32, name=f"acc{i}") for i in range(TILES)]
 
@@ -67,7 +67,7 @@ def tile_mix_xres_tm_relu2_kernel(tc, x4_words, x4_scales, xr, w4_words, w4_scal
         landed = {}
 
         def load_xr(a, first, end):
-            raw = keep.tile([P, PACK, P * (end - first)], F32, name=f"raw{a}_{first}", align_bytes=64)
+            raw = keep.tile([P, PACK, P * (end - first)], F32, name=f"raw{a}_{first}", align_bytes=256)
             rows = xr[K_PASS * a : K_PASS * (a + 1), P * first : P * end]
             nc.sync.dma_start(out=raw[:], in_=rows.rearrange("(p j) t -> p j t", j=PACK))
             for i in range(first, end):

@@ -22,11 +22,6 @@ TILES = T // P
 QUADRANT = 32
 WARM_UP_PASSES = 4
 
-XR_LOADS = (
-    (0, 0, 8), (1, 0, 4), (2, 0, 2), (2, 2, 4),
-    (1, 4, 6), (2, 4, 6), (1, 6, 8), (2, 6, 7), (2, 7, 8),
-)
-
 
 def tile_mix_xres_tm_relu2_kernel(tc, x4_words, x4_scales, xr, w4_words, w4_scales, out):
     nc = tc.nc
@@ -43,7 +38,7 @@ def tile_mix_xres_tm_relu2_kernel(tc, x4_words, x4_scales, xr, w4_words, w4_scal
         codes = [keep.tile([P, T], U32, name=f"codes{a}", align_bytes=256) for a in range(PASSES)]
         xr_plane = [keep.tile([P, T], U8, name=f"xr_plane{a}", align_bytes=256) for a in range(PASSES)]
         positive = [keep.tile([P, N], F32, name=f"positive{i}", align_bytes=256) for i in range(TILES)]
-        result = [keep.tile([P, N], F32, name=f"result{i}", align_bytes=256) for i in range(TILES)]
+        result = keep.tile([P, TILES, N], F32, name="result", align_bytes=256)
         table_probe = keep.tile([P, 1], F32, name="table_probe")
         acc = [psum.tile([P, N], F32, name=f"acc{i}") for i in range(TILES)]
 
@@ -51,10 +46,17 @@ def tile_mix_xres_tm_relu2_kernel(tc, x4_words, x4_scales, xr, w4_words, w4_scal
         nc.vector.memset(x4_plane[:].rearrange("p a n -> p (a n)").bitcast(I32), 0)
         nc.gpsimd.memset(table_probe[:], 0.0)
 
-        def load_words(tile, words, first, end):
+        def load_w4(first, end):
             nc.sync.dma_start(
-                out=tile[:, first:end, :].bitcast(I32),
-                in_=words[first:end].rearrange("a p n -> p a n").bitcast(I32),
+                out=w4[:, first:end, :].bitcast(I32),
+                in_=w4_words[first:end].rearrange("a p n -> p a n").bitcast(I32),
+            )
+
+        def load_x4(first_pass, end_pass, first=0, end=TILES):
+            cols = slice(2 * P * first, 2 * P * end)
+            nc.sync.dma_start(
+                out=x4[:, first_pass:end_pass, cols].bitcast(I32),
+                in_=x4_words[first_pass:end_pass, :, cols].rearrange("a p n -> p a n").bitcast(I32),
             )
 
         def load_scales(plane, scales, rows):
@@ -63,6 +65,12 @@ def tile_mix_xres_tm_relu2_kernel(tc, x4_words, x4_scales, xr, w4_words, w4_scal
                     out=plane[:].bitcast(I32)[r:P:QUADRANT, :, :],
                     in_=scales[:, r:16:4, :].rearrange("a g n -> g a n").bitcast(I32),
                 )
+
+        def load_w4_scales(rows):
+            load_scales(w4_plane, w4_scales, rows)
+
+        def load_x4_scales(rows):
+            load_scales(x4_plane, x4_scales, rows)
 
         landed = {}
 
@@ -99,123 +107,113 @@ def tile_mix_xres_tm_relu2_kernel(tc, x4_words, x4_scales, xr, w4_words, w4_scal
                 stop=stop,
             )
 
+        added = [0] * TILES
+
+        def add_pass(i, a, lhsT, lhsT_scale):
+            mx_pass(acc[i], a, lhsT, lhsT_scale, start=(added[i] == 0), stop=(added[i] == 2 * PASSES - 1))
+            added[i] = added[i] + 1
+
         def x4_passes(a, first, end):
             for i in range(first, end):
                 words = x4[:, a, 2 * P * i : 2 * P * (i + 1)].bitcast(FP4X4)
-                mx_pass(acc[i], a, words, x4_plane[:, a, P * i : P * (i + 1)], start=(a == 0), stop=False)
+                add_pass(i, a, words, x4_plane[:, a, P * i : P * (i + 1)])
 
         def xr_passes(a, first, end):
             for i in range(first, end):
                 cols = slice(P * i, P * (i + 1))
-                words = codes[a][:, cols].bitcast(FP8X4)
-                mx_pass(acc[i], a, words, xr_plane[a][:, cols], start=False, stop=(a == PASSES - 1))
+                add_pass(i, a, codes[a][:, cols].bitcast(FP8X4), xr_plane[a][:, cols])
 
         def quantize_and_multiply(a, first, end):
             quantize(a, first, end)
             xr_passes(a, first, end)
 
+        def warm_up(passes):
+            for repeat in range(passes):
+                mx_pass(acc[TILES - 1], 0, w4[:, 0, : 2 * P].bitcast(FP4X4), w4_plane[:, 0, :P], start=True, stop=True)
+
         whole = slice(0, N)
         halves = (slice(0, N // 2), slice(N // 2, N))
-
-        def scalar_relu(i, cols=whole):
-            nc.scalar.activation(out=positive[i][:, cols], in_=acc[i][:, cols], func=ACT.Relu)
-
-        def scalar_square(i, cols=whole):
-            nc.scalar.activation(out=result[i][:, cols], in_=positive[i][:, cols], func=ACT.Square)
-
-        def vector_relu(i, cols=whole):
-            nc.vector.tensor_scalar_max(out=positive[i][:, cols], in0=acc[i][:, cols], scalar1=0.0)
-
-        def vector_square(i, cols=whole):
-            nc.vector.tensor_mul(out=result[i][:, cols], in0=positive[i][:, cols], in1=positive[i][:, cols])
-
-        def scalar_finish(first, end):
-            for i in range(first, end):
-                scalar_relu(i)
-            for i in range(first, end):
-                scalar_square(i)
-                store(i)
-
-        def store(i, cols=whole):
-            nc.sync.dma_start(out=out[P * i : P * (i + 1), cols], in_=result[i][:, cols])
-
+        quarters = [slice(q * N // 4, (q + 1) * N // 4) for q in range(4)]
         on_vector, on_scalar = nc.vector.tensor_copy, nc.scalar.copy
+
+        def relu(engine, i, cols=whole):
+            if engine is on_vector:
+                nc.vector.tensor_scalar_max(out=positive[i][:, cols], in0=acc[i][:, cols], scalar1=0.0)
+            else:
+                nc.scalar.activation(out=positive[i][:, cols], in_=acc[i][:, cols], func=ACT.Relu)
+
+        def square(engine, i, cols=whole):
+            if engine is on_vector:
+                nc.vector.tensor_mul(out=result[:, i, cols], in0=positive[i][:, cols], in1=positive[i][:, cols])
+            else:
+                nc.scalar.activation(out=result[:, i, cols], in_=positive[i][:, cols], func=ACT.Square)
+
+        def store(first, end, cols=whole):
+            rows = out[P * first : P * end, cols].rearrange("(i p) n -> p i n", p=P)
+            nc.sync.dma_start(out=rows, in_=result[:, first:end, cols])
 
         nc.scalar.activation(out=table_probe[:], in_=table_probe[:], func=ACT.Relu)
 
-        load_words(w4, w4_words, 0, 3)
-        load_scales(w4_plane, w4_scales, range(0, 4))
-        load_scales(x4_plane, x4_scales, range(0, 2))
-        load_words(x4, x4_words, 0, 2)
-        load_scales(x4_plane, x4_scales, range(2, 4))
-        load_words(x4, x4_words, 2, 3)
-        for a, first, end in XR_LOADS:
+        load_w4(0, 3)
+        load_w4_scales(range(0, 4))
+        load_x4_scales(range(0, 2))
+        load_x4(0, 2)
+        load_x4_scales(range(2, 4))
+        load_x4(2, 3)
+        for a, first, end in ((0, 0, 4), (1, 0, 4), (2, 0, 2), (2, 2, 4), (0, 4, 6), (1, 4, 6), (2, 4, 6), (0, 6, 8), (1, 6, 7), (2, 6, 7), (1, 7, 8), (2, 7, 8)):
             load_xr(a, first, end)
-
-        for repeat in range(WARM_UP_PASSES):
-            mx_pass(acc[TILES - 1], 0, w4[:, 0, : 2 * P].bitcast(FP4X4), w4_plane[:, 0, :P], start=True, stop=True)
-        x4_passes(0, 0, 8)
-        x4_passes(1, 0, 8)
-        x4_passes(2, 0, 6)
-        interleave(on_vector, 0, 0, 2)
-        interleave(on_scalar, 0, 4, 6)
-        interleave(on_vector, 0, 2, 4)
-        quantize_and_multiply(0, 0, 2)
-        quantize_and_multiply(0, 2, 4)
-        interleave(on_scalar, 0, 6, 8)
-        quantize(0, 4, 6)
-        interleave(on_vector, 1, 0, 1)
-        interleave(on_vector, 1, 1, 2)
-        interleave(on_scalar, 1, 2, 4)
-        quantize_and_multiply(1, 0, 1)
-        quantize_and_multiply(1, 1, 2)
-        xr_passes(0, 4, 5)
-        interleave(on_vector, 2, 0, 1)
-        interleave(on_scalar, 2, 1, 2)
-        quantize(1, 2, 4)
-        quantize_and_multiply(2, 0, 1)
-        quantize_and_multiply(2, 1, 2)
-        xr_passes(1, 2, 4)
-        quantize(0, 6, 8)
-        interleave(on_vector, 2, 2, 3)
-        interleave(on_vector, 2, 3, 4)
-        quantize_and_multiply(2, 2, 3)
-        quantize_and_multiply(2, 3, 4)
-        xr_passes(0, 5, 8)
+        warm_up(4)
+        for a in range(3):
+            x4_passes(a, 0, 4)
+        x4_passes(0, 4, 6)
+        for a in range(2):
+            interleave(on_vector, a, 0, 1)
+            interleave(on_scalar, a, 2, 3)
+            interleave(on_vector, a, 1, 2)
+            interleave(on_scalar, a, 3, 4)
+            for i in range(4):
+                quantize_and_multiply(a, i, i + 1)
+            if a == 0:
+                x4_passes(0, 6, 6)
+                x4_passes(1, 4, 6)
+        for i in (0, 2):
+            interleave(on_vector, 2, i, i + 1)
+            interleave(on_scalar, 2, i + 1, i + 2)
+            quantize_and_multiply(2, i, i + 1)
+            quantize_and_multiply(2, i + 1, i + 2)
+        x4_passes(2, 4, 6)
+        for i in (0, 2):
+            relu(on_scalar,i); relu(on_scalar,i+1); square(on_scalar,i); store(i,i+1); square(on_scalar,i+1); store(i+1,i+2)
+        interleave(on_vector, 0, 4, 5)
+        for a in range(3):
+            interleave(on_vector, a, 5, 6)
+            quantize_and_multiply(a, 4, 5)
+            if a < 2:
+                x4_passes(a, 6, 7)
+                interleave(on_vector, a + 1, 4, 5)
+            quantize_and_multiply(a, 5, 6)
+            if a < 2:
+                x4_passes(a, 7, 8)
         x4_passes(2, 6, 8)
-        scalar_finish(0, 2)
-        interleave(on_vector, 1, 4, 6)
-        vector_relu(2)
-        quantize_and_multiply(1, 4, 6)
-        scalar_relu(3)
-        scalar_square(2)
-        store(2)
-        scalar_square(3)
-        store(3)
-        interleave(on_vector, 2, 4, 5)
-        interleave(on_vector, 2, 5, 6)
-        quantize_and_multiply(2, 4, 5)
-        quantize_and_multiply(2, 5, 6)
-        interleave(on_vector, 1, 6, 8)
+        relu(on_scalar,4); relu(on_scalar,5); square(on_scalar,4); store(4,5); square(on_scalar,5); store(5,6)
+        interleave(on_vector, 0, 6, 7)
+        interleave(on_vector, 0, 7, 8)
+        quantize_and_multiply(0, 6, 7)
+        interleave(on_vector, 1, 6, 7)
+        quantize_and_multiply(0, 7, 8)
         interleave(on_vector, 2, 6, 7)
         quantize_and_multiply(1, 6, 7)
         quantize_and_multiply(2, 6, 7)
+        interleave(on_vector, 1, 7, 8)
         interleave(on_vector, 2, 7, 8)
         quantize_and_multiply(1, 7, 8)
         quantize_and_multiply(2, 7, 8)
-        scalar_relu(4)
-        scalar_relu(5)
-        scalar_square(4)
-        store(4)
-        scalar_square(5)
-        store(5)
         for cols in halves:
-            vector_relu(6, cols)
+            relu(on_vector,6, cols)
         for cols in halves:
-            vector_relu(7, cols)
-        for cols in halves:
-            scalar_square(6, cols)
-        store(6)
-        for square, cols in zip((vector_square, scalar_square), halves):
-            square(7, cols)
-        store(7)
+            square(on_scalar,6, cols)
+        store(6,7)
+        for cols in quarters:
+            relu(on_vector,7, cols)
+        square(on_scalar,7,quarters[0]); square(on_scalar,7,quarters[1]); store(7,8,halves[0])
+        square(on_vector,7,quarters[2]); square(on_vector,7,quarters[3]); store(7,8,halves[1])

@@ -18,9 +18,18 @@ P = 128
 PACK = 4
 K_PASS = P * PACK
 PASSES = K // K_PASS
+LAST_PASS = PASSES - 1
 TILES = T // P
 QUADRANT = 32
+SCALE_ROWS = 16
+ALIGN = 256
 WARM_UP_PASSES = 4
+
+XR_LOADS = (
+    (0, 0, 4), (1, 0, 4), (2, 0, 2), (2, 2, 4),
+    (0, 4, 6), (1, 4, 6), (2, 4, 6),
+    (0, 6, 8), (1, 6, 7), (2, 6, 7), (1, 7, 8), (2, 7, 8),
+)
 
 
 def tile_mix_xres_tm_relu2_kernel(tc, x4_words, x4_scales, xr, w4_words, w4_scales, out):
@@ -30,15 +39,15 @@ def tile_mix_xres_tm_relu2_kernel(tc, x4_words, x4_scales, xr, w4_words, w4_scal
         psum = ctx.enter_context(tc.psum_pool(name="psum", bufs=1))
         ctx.enter_context(tc.manual_schedule())
 
-        w4 = keep.tile([P, PASSES, 2 * N], U8, name="w4", align_bytes=256)
-        w4_plane = keep.tile([P, PASSES, N], U8, name="w4_plane", align_bytes=256)
-        x4 = keep.tile([P, PASSES, 2 * T], U8, name="x4", align_bytes=256)
-        x4_plane = keep.tile([P, PASSES, T], U8, name="x4_plane", align_bytes=256)
-        rounded = [keep.tile([P, T, PACK], BF16, name=f"rounded{a}", align_bytes=256) for a in range(PASSES)]
-        codes = [keep.tile([P, T], U32, name=f"codes{a}", align_bytes=256) for a in range(PASSES)]
-        xr_plane = [keep.tile([P, T], U8, name=f"xr_plane{a}", align_bytes=256) for a in range(PASSES)]
-        positive = [keep.tile([P, N], F32, name=f"positive{i}", align_bytes=256) for i in range(TILES)]
-        result = keep.tile([P, TILES, N], F32, name="result", align_bytes=256)
+        w4 = keep.tile([P, PASSES, 2 * N], U8, name="w4", align_bytes=ALIGN)
+        w4_plane = keep.tile([P, PASSES, N], U8, name="w4_plane", align_bytes=ALIGN)
+        x4 = keep.tile([P, PASSES, 2 * T], U8, name="x4", align_bytes=ALIGN)
+        x4_plane = keep.tile([P, PASSES, T], U8, name="x4_plane", align_bytes=ALIGN)
+        rounded = [keep.tile([P, T, PACK], BF16, name=f"rounded{a}", align_bytes=ALIGN) for a in range(PASSES)]
+        codes = [keep.tile([P, T], U32, name=f"codes{a}", align_bytes=ALIGN) for a in range(PASSES)]
+        xr_plane = [keep.tile([P, T], U8, name=f"xr_plane{a}", align_bytes=ALIGN) for a in range(PASSES)]
+        positive = [keep.tile([P, N], F32, name=f"positive{i}", align_bytes=ALIGN) for i in range(TILES)]
+        result = keep.tile([P, TILES, N], F32, name="result", align_bytes=ALIGN)
         table_probe = keep.tile([P, 1], F32, name="table_probe")
         acc = [psum.tile([P, N], F32, name=f"acc{i}") for i in range(TILES)]
 
@@ -46,54 +55,35 @@ def tile_mix_xres_tm_relu2_kernel(tc, x4_words, x4_scales, xr, w4_words, w4_scal
         nc.vector.memset(x4_plane[:].rearrange("p a n -> p (a n)").bitcast(I32), 0)
         nc.gpsimd.memset(table_probe[:], 0.0)
 
-        def load_w4(first, end):
+        def load_words(tile, words, first_pass, end_pass):
             nc.sync.dma_start(
-                out=w4[:, first:end, :].bitcast(I32),
-                in_=w4_words[first:end].rearrange("a p n -> p a n").bitcast(I32),
-            )
-
-        def load_x4(first_pass, end_pass, first=0, end=TILES):
-            cols = slice(2 * P * first, 2 * P * end)
-            nc.sync.dma_start(
-                out=x4[:, first_pass:end_pass, cols].bitcast(I32),
-                in_=x4_words[first_pass:end_pass, :, cols].rearrange("a p n -> p a n").bitcast(I32),
+                out=tile[:, first_pass:end_pass, :].bitcast(I32),
+                in_=words[first_pass:end_pass].rearrange("a p n -> p a n").bitcast(I32),
             )
 
         def load_scales(plane, scales, rows):
             for r in rows:
                 nc.sync.dma_start(
                     out=plane[:].bitcast(I32)[r:P:QUADRANT, :, :],
-                    in_=scales[:, r:16:4, :].rearrange("a g n -> g a n").bitcast(I32),
+                    in_=scales[:, r:SCALE_ROWS:4, :].rearrange("a g n -> g a n").bitcast(I32),
                 )
-
-        def load_w4_scales(rows):
-            load_scales(w4_plane, w4_scales, rows)
-
-        def load_x4_scales(rows):
-            load_scales(x4_plane, x4_scales, rows)
 
         landed = {}
 
         def load_xr(a, first, end):
-            raw = keep.tile([P, PACK, P * (end - first)], F32, name=f"raw{a}_{first}", align_bytes=256)
+            raw = keep.tile([P, PACK, P * (end - first)], F32, name=f"raw{a}_{first}", align_bytes=ALIGN)
             rows = xr[K_PASS * a : K_PASS * (a + 1), P * first : P * end]
             nc.sync.dma_start(out=raw[:], in_=rows.rearrange("(p j) t -> p j t", j=PACK))
             for i in range(first, end):
                 landed[a, i] = (raw, P * (i - first))
 
-        def interleave(copy, a, first, end):
-            raw, t0 = landed[a, first]
-            copy(
-                out=rounded[a][:, P * first : P * end, :].rearrange("p (c i) j -> p c j i", i=4),
-                in_=raw[:, :, t0 : t0 + P * (end - first)].rearrange("p j (c i) -> p c j i", i=4),
-            )
+        on_vector, on_scalar = nc.vector.tensor_copy, nc.scalar.copy
 
-        def quantize(a, first, end):
-            cols = slice(P * first, P * end)
-            nc.vector.quantize_mx(
-                out=codes[a][:, cols].bitcast(FP8X4),
-                scales=xr_plane[a][:, cols],
-                in_=rounded[a][:, cols, :].rearrange("p t j -> p (t j)"),
+        def interleave(copy, a, i):
+            raw, t0 = landed[a, i]
+            copy(
+                out=rounded[a][:, P * i : P * (i + 1), :].rearrange("p (c e) j -> p c j e", e=4),
+                in_=raw[:, :, t0 : t0 + P].rearrange("p j (c e) -> p c j e", e=4),
             )
 
         def mx_pass(bank, a, lhsT, lhsT_scale, start, stop):
@@ -107,113 +97,119 @@ def tile_mix_xres_tm_relu2_kernel(tc, x4_words, x4_scales, xr, w4_words, w4_scal
                 stop=stop,
             )
 
-        added = [0] * TILES
-
-        def add_pass(i, a, lhsT, lhsT_scale):
-            mx_pass(acc[i], a, lhsT, lhsT_scale, start=(added[i] == 0), stop=(added[i] == 2 * PASSES - 1))
-            added[i] = added[i] + 1
-
         def x4_passes(a, first, end):
             for i in range(first, end):
                 words = x4[:, a, 2 * P * i : 2 * P * (i + 1)].bitcast(FP4X4)
-                add_pass(i, a, words, x4_plane[:, a, P * i : P * (i + 1)])
+                mx_pass(acc[i], a, words, x4_plane[:, a, P * i : P * (i + 1)], start=(a == 0), stop=False)
 
-        def xr_passes(a, first, end):
-            for i in range(first, end):
-                cols = slice(P * i, P * (i + 1))
-                add_pass(i, a, codes[a][:, cols].bitcast(FP8X4), xr_plane[a][:, cols])
-
-        def quantize_and_multiply(a, first, end):
-            quantize(a, first, end)
-            xr_passes(a, first, end)
-
-        def warm_up(passes):
-            for repeat in range(passes):
-                mx_pass(acc[TILES - 1], 0, w4[:, 0, : 2 * P].bitcast(FP4X4), w4_plane[:, 0, :P], start=True, stop=True)
+        def quantize_and_multiply(a, i):
+            cols = slice(P * i, P * (i + 1))
+            nc.vector.quantize_mx(
+                out=codes[a][:, cols].bitcast(FP8X4),
+                scales=xr_plane[a][:, cols],
+                in_=rounded[a][:, cols, :].rearrange("p t j -> p (t j)"),
+            )
+            mx_pass(acc[i], a, codes[a][:, cols].bitcast(FP8X4), xr_plane[a][:, cols], start=False, stop=(a == LAST_PASS))
 
         whole = slice(0, N)
-        halves = (slice(0, N // 2), slice(N // 2, N))
-        quarters = [slice(q * N // 4, (q + 1) * N // 4) for q in range(4)]
-        on_vector, on_scalar = nc.vector.tensor_copy, nc.scalar.copy
+        halves = [slice(h * N // 2, (h + 1) * N // 2) for h in range(2)]
+        quarters = [slice(h * N // 4, (h + 1) * N // 4) for h in range(4)]
 
-        def relu(engine, i, cols=whole):
-            if engine is on_vector:
-                nc.vector.tensor_scalar_max(out=positive[i][:, cols], in0=acc[i][:, cols], scalar1=0.0)
-            else:
-                nc.scalar.activation(out=positive[i][:, cols], in_=acc[i][:, cols], func=ACT.Relu)
+        def scalar_relu(i, cols=whole):
+            nc.scalar.activation(out=positive[i][:, cols], in_=acc[i][:, cols], func=ACT.Relu)
 
-        def square(engine, i, cols=whole):
-            if engine is on_vector:
-                nc.vector.tensor_mul(out=result[:, i, cols], in0=positive[i][:, cols], in1=positive[i][:, cols])
-            else:
-                nc.scalar.activation(out=result[:, i, cols], in_=positive[i][:, cols], func=ACT.Square)
+        def scalar_square(i, cols=whole):
+            nc.scalar.activation(out=result[:, i, cols], in_=positive[i][:, cols], func=ACT.Square)
 
-        def store(first, end, cols=whole):
-            rows = out[P * first : P * end, cols].rearrange("(i p) n -> p i n", p=P)
-            nc.sync.dma_start(out=rows, in_=result[:, first:end, cols])
+        def vector_relu(i, cols):
+            nc.vector.tensor_scalar_max(out=positive[i][:, cols], in0=acc[i][:, cols], scalar1=0.0)
+
+        def vector_square(i, cols):
+            nc.vector.tensor_mul(out=result[:, i, cols], in0=positive[i][:, cols], in1=positive[i][:, cols])
+
+        def store(i, cols=whole):
+            rows = out[P * i : P * (i + 1), cols].rearrange("(i p) n -> p i n", p=P)
+            nc.sync.dma_start(out=rows, in_=result[:, i : i + 1, cols])
+
+        def scalar_finish_pair(first):
+            for i in (first, first + 1):
+                scalar_relu(i)
+            for i in (first, first + 1):
+                scalar_square(i)
+                store(i)
 
         nc.scalar.activation(out=table_probe[:], in_=table_probe[:], func=ACT.Relu)
 
-        load_w4(0, 3)
-        load_w4_scales(range(0, 4))
-        load_x4_scales(range(0, 2))
-        load_x4(0, 2)
-        load_x4_scales(range(2, 4))
-        load_x4(2, 3)
-        for a, first, end in ((0, 0, 4), (1, 0, 4), (2, 0, 2), (2, 2, 4), (0, 4, 6), (1, 4, 6), (2, 4, 6), (0, 6, 8), (1, 6, 7), (2, 6, 7), (1, 7, 8), (2, 7, 8)):
+        load_words(w4, w4_words, 0, PASSES)
+        load_scales(w4_plane, w4_scales, range(0, 4))
+        load_scales(x4_plane, x4_scales, range(0, 2))
+        load_words(x4, x4_words, 0, PASSES)
+        load_scales(x4_plane, x4_scales, range(2, 4))
+        for a, first, end in XR_LOADS:
             load_xr(a, first, end)
-        warm_up(4)
-        for a in range(3):
+
+        for repeat in range(WARM_UP_PASSES):
+            mx_pass(acc[TILES - 1], 0, w4[:, 0, : 2 * P].bitcast(FP4X4), w4_plane[:, 0, :P], start=True, stop=True)
+
+        for a in range(PASSES):
             x4_passes(a, 0, 4)
         x4_passes(0, 4, 6)
-        for a in range(2):
-            interleave(on_vector, a, 0, 1)
-            interleave(on_scalar, a, 2, 3)
-            interleave(on_vector, a, 1, 2)
-            interleave(on_scalar, a, 3, 4)
+        for a in range(LAST_PASS):
+            for i in (0, 1):
+                interleave(on_vector, a, i)
+                interleave(on_scalar, a, i + 2)
             for i in range(4):
-                quantize_and_multiply(a, i, i + 1)
+                quantize_and_multiply(a, i)
             if a == 0:
-                x4_passes(0, 6, 6)
                 x4_passes(1, 4, 6)
-        for i in (0, 2):
-            interleave(on_vector, 2, i, i + 1)
-            interleave(on_scalar, 2, i + 1, i + 2)
-            quantize_and_multiply(2, i, i + 1)
-            quantize_and_multiply(2, i + 1, i + 2)
-        x4_passes(2, 4, 6)
-        for i in (0, 2):
-            relu(on_scalar,i); relu(on_scalar,i+1); square(on_scalar,i); store(i,i+1); square(on_scalar,i+1); store(i+1,i+2)
-        interleave(on_vector, 0, 4, 5)
-        for a in range(3):
-            interleave(on_vector, a, 5, 6)
-            quantize_and_multiply(a, 4, 5)
-            if a < 2:
+        for first in (0, 2):
+            interleave(on_vector, LAST_PASS, first)
+            interleave(on_scalar, LAST_PASS, first + 1)
+            quantize_and_multiply(LAST_PASS, first)
+            quantize_and_multiply(LAST_PASS, first + 1)
+        x4_passes(LAST_PASS, 4, 6)
+        for first in (0, 2):
+            scalar_finish_pair(first)
+
+        interleave(on_vector, 0, 4)
+        for a in range(PASSES):
+            interleave(on_vector, a, 5)
+            quantize_and_multiply(a, 4)
+            if a < LAST_PASS:
                 x4_passes(a, 6, 7)
-                interleave(on_vector, a + 1, 4, 5)
-            quantize_and_multiply(a, 5, 6)
-            if a < 2:
+                interleave(on_vector, a + 1, 4)
+            quantize_and_multiply(a, 5)
+            if a < LAST_PASS:
                 x4_passes(a, 7, 8)
-        x4_passes(2, 6, 8)
-        relu(on_scalar,4); relu(on_scalar,5); square(on_scalar,4); store(4,5); square(on_scalar,5); store(5,6)
-        interleave(on_vector, 0, 6, 7)
-        interleave(on_vector, 0, 7, 8)
-        quantize_and_multiply(0, 6, 7)
-        interleave(on_vector, 1, 6, 7)
-        quantize_and_multiply(0, 7, 8)
-        interleave(on_vector, 2, 6, 7)
-        quantize_and_multiply(1, 6, 7)
-        quantize_and_multiply(2, 6, 7)
-        interleave(on_vector, 1, 7, 8)
-        interleave(on_vector, 2, 7, 8)
-        quantize_and_multiply(1, 7, 8)
-        quantize_and_multiply(2, 7, 8)
-        for cols in halves:
-            relu(on_vector,6, cols)
-        for cols in halves:
-            square(on_scalar,6, cols)
-        store(6,7)
+        x4_passes(LAST_PASS, 6, 8)
+        for i in (4, 5):
+            for cols in halves:
+                scalar_relu(i, cols)
+            for cols in halves:
+                scalar_square(i, cols)
+            store(i)
+
+        interleave(on_vector, 0, 6)
+        interleave(on_vector, 0, 7)
+        quantize_and_multiply(0, 6)
+        interleave(on_vector, 1, 6)
+        quantize_and_multiply(0, 7)
+        interleave(on_vector, LAST_PASS, 6)
+        quantize_and_multiply(1, 6)
+        quantize_and_multiply(LAST_PASS, 6)
+        for a in (1, LAST_PASS):
+            interleave(on_vector, a, 7)
+        for a in (1, LAST_PASS):
+            quantize_and_multiply(a, 7)
+
         for cols in quarters:
-            relu(on_vector,7, cols)
-        square(on_scalar,7,quarters[0]); square(on_scalar,7,quarters[1]); store(7,8,halves[0])
-        square(on_vector,7,quarters[2]); square(on_vector,7,quarters[3]); store(7,8,halves[1])
+            vector_relu(6, cols)
+        for cols in quarters:
+            scalar_square(6, cols)
+        store(6)
+        for cols in quarters:
+            vector_relu(7, cols)
+        for h, square in enumerate((scalar_square, vector_square)):
+            for cols in quarters[2 * h : 2 * h + 2]:
+                square(7, cols)
+            store(7, halves[h])

@@ -127,9 +127,9 @@ def tile_mix_xres_tm_relu2_kernel(tc, x4_words, x4_scales, xr, w4_words, w4_scal
         def vector_square(i, cols):
             nc.vector.tensor_mul(out=result[:, i, cols], in0=positive[i][:, cols], in1=positive[i][:, cols])
 
-        def store(i, cols=whole):
-            rows = out[P * i : P * (i + 1), cols].rearrange("(i p) n -> p i n", p=P)
-            nc.sync.dma_start(out=rows, in_=result[:, i : i + 1, cols])
+        def store(i):
+            rows = out[P * i : P * (i + 1), :].rearrange("(i p) n -> p i n", p=P)
+            nc.sync.dma_start(out=rows, in_=result[:, i : i + 1, :])
 
         def scalar_finish_pair(first):
             for i in (first, first + 1):
@@ -212,4 +212,4 @@ def tile_mix_xres_tm_relu2_kernel(tc, x4_words, x4_scales, xr, w4_words, w4_scal
         for h, square in enumerate((scalar_square, vector_square)):
             for cols in quarters[2 * h : 2 * h + 2]:
                 square(7, cols)
-            store(7, halves[h])
+        store(7)

@@ -79,11 +79,11 @@ def tile_mix_xres_tm_relu2_kernel(tc, x4_words, x4_scales, xr, w4_words, w4_scal
 
         on_vector, on_scalar = nc.vector.tensor_copy, nc.scalar.copy
 
-        def interleave(copy, a, i):
-            raw, t0 = landed[a, i]
+        def interleave(copy, a, first, tiles=1):
+            raw, t0 = landed[a, first]
             copy(
-                out=rounded[a][:, P * i : P * (i + 1), :].rearrange("p (c e) j -> p c j e", e=4),
-                in_=raw[:, :, t0 : t0 + P].rearrange("p j (c e) -> p c j e", e=4),
+                out=rounded[a][:, P * first : P * (first + tiles), :].rearrange("p (c e) j -> p c j e", e=4),
+                in_=raw[:, :, t0 : t0 + P * tiles].rearrange("p j (c e) -> p c j e", e=4),
             )
 
         def mx_pass(bank, a, lhsT, lhsT_scale, start, stop):
@@ -102,14 +102,22 @@ def tile_mix_xres_tm_relu2_kernel(tc, x4_words, x4_scales, xr, w4_words, w4_scal
                 words = x4[:, a, 2 * P * i : 2 * P * (i + 1)].bitcast(FP4X4)
                 mx_pass(acc[i], a, words, x4_plane[:, a, P * i : P * (i + 1)], start=(a == 0), stop=False)
 
-        def quantize_and_multiply(a, i):
-            cols = slice(P * i, P * (i + 1))
+        def quantize(a, first, tiles=1):
+            cols = slice(P * first, P * (first + tiles))
             nc.vector.quantize_mx(
                 out=codes[a][:, cols].bitcast(FP8X4),
                 scales=xr_plane[a][:, cols],
                 in_=rounded[a][:, cols, :].rearrange("p t j -> p (t j)"),
             )
+
+        def xr_pass(a, i):
+            cols = slice(P * i, P * (i + 1))
             mx_pass(acc[i], a, codes[a][:, cols].bitcast(FP8X4), xr_plane[a][:, cols], start=False, stop=(a == LAST_PASS))
+
+        def quantize_and_multiply(a, first, tiles=1):
+            quantize(a, first, tiles)
+            for i in range(first, first + tiles):
+                xr_pass(a, i)
 
         whole = slice(0, N)
         halves = [slice(h * N // 2, (h + 1) * N // 2) for h in range(2)]
@@ -127,16 +135,12 @@ def tile_mix_xres_tm_relu2_kernel(tc, x4_words, x4_scales, xr, w4_words, w4_scal
         def vector_square(i, cols):
             nc.vector.tensor_mul(out=result[:, i, cols], in0=positive[i][:, cols], in1=positive[i][:, cols])
 
-        def store(i):
-            rows = out[P * i : P * (i + 1), :].rearrange("(i p) n -> p i n", p=P)
-            nc.sync.dma_start(out=rows, in_=result[:, i : i + 1, :])
+        def gpsimd_square(i, cols):
+            nc.gpsimd.tensor_mul(out=result[:, i, cols], in0=positive[i][:, cols], in1=positive[i][:, cols])
 
-        def scalar_finish_pair(first):
-            for i in (first, first + 1):
-                scalar_relu(i)
-            for i in (first, first + 1):
-                scalar_square(i)
-                store(i)
+        def store(first, end):
+            rows = out[P * first : P * end, :].rearrange("(i p) n -> p i n", p=P)
+            nc.sync.dma_start(out=rows, in_=result[:, first:end, :])
 
         nc.scalar.activation(out=table_probe[:], in_=table_probe[:], func=ACT.Relu)
 
@@ -151,65 +155,89 @@ def tile_mix_xres_tm_relu2_kernel(tc, x4_words, x4_scales, xr, w4_words, w4_scal
         for repeat in range(WARM_UP_PASSES):
             mx_pass(acc[TILES - 1], 0, w4[:, 0, : 2 * P].bitcast(FP4X4), w4_plane[:, 0, :P], start=True, stop=True)
 
-        for a in range(PASSES):
-            x4_passes(a, 0, 4)
-        x4_passes(0, 4, 6)
-        for a in range(LAST_PASS):
-            for i in (0, 1):
-                interleave(on_vector, a, i)
-                interleave(on_scalar, a, i + 2)
-            for i in range(4):
-                quantize_and_multiply(a, i)
-            if a == 0:
-                x4_passes(1, 4, 6)
-        for first in (0, 2):
-            interleave(on_vector, LAST_PASS, first)
-            interleave(on_scalar, LAST_PASS, first + 1)
-            quantize_and_multiply(LAST_PASS, first)
-            quantize_and_multiply(LAST_PASS, first + 1)
-        x4_passes(LAST_PASS, 4, 6)
-        for first in (0, 2):
-            scalar_finish_pair(first)
-
+        x4_passes(0, 0, 4)
+        x4_passes(1, 0, 4)
+        x4_passes(2, 0, 4)
+        x4_passes(0, 4, 5)
+        interleave(on_vector, 0, 0)
+        interleave(on_scalar, 0, 2)
+        interleave(on_vector, 0, 1)
+        interleave(on_scalar, 0, 3)
+        quantize_and_multiply(0, 0)
+        quantize_and_multiply(0, 1)
+        quantize_and_multiply(0, 2)
+        quantize_and_multiply(0, 3)
+        x4_passes(0, 5, 6)
+        interleave(on_vector, 1, 0)
+        interleave(on_scalar, 1, 2)
+        interleave(on_vector, 1, 1)
+        interleave(on_scalar, 1, 3)
+        quantize_and_multiply(1, 0)
+        quantize_and_multiply(1, 1)
+        quantize_and_multiply(1, 2)
+        interleave(on_vector, 2, 0)
+        quantize_and_multiply(1, 3)
+        interleave(on_scalar, 2, 1)
+        quantize_and_multiply(2, 0)
+        quantize_and_multiply(2, 1)
+        interleave(on_vector, 2, 2)
+        interleave(on_scalar, 2, 3)
+        quantize_and_multiply(2, 2)
+        quantize_and_multiply(2, 3)
+        x4_passes(1, 4, 6)
+        x4_passes(2, 4, 6)
+        scalar_relu(0)
+        scalar_relu(1)
+        scalar_square(0)
+        scalar_square(1)
+        store(0, 2)
+        scalar_relu(2)
+        scalar_relu(3)
+        scalar_square(2)
+        scalar_square(3)
+        store(2, 4)
         interleave(on_vector, 0, 4)
-        for a in range(PASSES):
-            interleave(on_vector, a, 5)
-            quantize_and_multiply(a, 4)
-            if a < LAST_PASS:
-                x4_passes(a, 6, 7)
-                interleave(on_vector, a + 1, 4)
-            quantize_and_multiply(a, 5)
-            if a < LAST_PASS:
-                x4_passes(a, 7, 8)
-        x4_passes(LAST_PASS, 6, 8)
-        for i in (4, 5):
-            for cols in halves:
-                scalar_relu(i, cols)
-            for cols in halves:
-                scalar_square(i, cols)
-            store(i)
-
+        interleave(on_vector, 0, 5)
+        quantize_and_multiply(0, 4)
+        interleave(on_vector, 1, 4)
+        quantize_and_multiply(0, 5)
+        x4_passes(0, 6, 8)
+        interleave(on_vector, 1, 5)
+        quantize_and_multiply(1, 4)
+        interleave(on_vector, 2, 4)
+        quantize_and_multiply(1, 5)
+        interleave(on_vector, 2, 5)
+        quantize_and_multiply(2, 4)
+        quantize_and_multiply(2, 5)
+        x4_passes(1, 6, 8)
+        x4_passes(2, 6, 7)
+        scalar_relu(4)
+        scalar_relu(5)
         interleave(on_vector, 0, 6)
         interleave(on_vector, 0, 7)
         quantize_and_multiply(0, 6)
         interleave(on_vector, 1, 6)
         quantize_and_multiply(0, 7)
-        interleave(on_vector, LAST_PASS, 6)
+        interleave(on_vector, 2, 6)
         quantize_and_multiply(1, 6)
-        quantize_and_multiply(LAST_PASS, 6)
-        for a in (1, LAST_PASS):
-            interleave(on_vector, a, 7)
-        for a in (1, LAST_PASS):
-            quantize_and_multiply(a, 7)
-
+        quantize_and_multiply(2, 6)
+        x4_passes(2, 7, 8)
+        interleave(on_scalar, 1, 7)
+        scalar_square(4)
+        store(4, 5)
+        scalar_square(5)
+        store(5, 6)
+        interleave(on_vector, 2, 7)
+        quantize_and_multiply(1, 7)
+        quantize_and_multiply(2, 7)
         for cols in quarters:
             vector_relu(6, cols)
         for cols in quarters:
             scalar_square(6, cols)
-        store(6)
+        store(6, 7)
         for cols in quarters:
             vector_relu(7, cols)
         for h, square in enumerate((scalar_square, vector_square)):
             for cols in quarters[2 * h : 2 * h + 2]:
                 square(7, cols)
-        store(7)
+        store(7, 8)

@@ -168,6 +168,7 @@ def tile_mix_xres_tm_relu2_kernel(tc, x4_words, x4_scales, xr, w4_words, w4_scal
         quantize_and_multiply(0, 2)
         quantize_and_multiply(0, 3)
         x4_passes(0, 5, 6)
+        x4_passes(1, 4, 5)
         interleave(on_vector, 1, 0)
         interleave(on_scalar, 1, 2)
         interleave(on_vector, 1, 1)
@@ -184,24 +185,28 @@ def tile_mix_xres_tm_relu2_kernel(tc, x4_words, x4_scales, xr, w4_words, w4_scal
         interleave(on_scalar, 2, 3)
         quantize_and_multiply(2, 2)
         quantize_and_multiply(2, 3)
-        x4_passes(1, 4, 6)
+        x4_passes(1, 5, 6)
         x4_passes(2, 4, 6)
+        x4_passes(0, 6, 7)
         scalar_relu(0)
         scalar_relu(1)
         scalar_square(0)
+        store(0, 1)
         scalar_square(1)
-        store(0, 2)
+        store(1, 2)
         scalar_relu(2)
         scalar_relu(3)
         scalar_square(2)
+        store(2, 3)
         scalar_square(3)
-        store(2, 4)
+        store(3, 4)
         interleave(on_vector, 0, 4)
         interleave(on_vector, 0, 5)
         quantize_and_multiply(0, 4)
         interleave(on_vector, 1, 4)
         quantize_and_multiply(0, 5)
-        x4_passes(0, 6, 8)
+        x4_passes(0, 7, 8)
+        x4_passes(1, 6, 7)
         interleave(on_vector, 1, 5)
         quantize_and_multiply(1, 4)
         interleave(on_vector, 2, 4)
@@ -209,10 +214,14 @@ def tile_mix_xres_tm_relu2_kernel(tc, x4_words, x4_scales, xr, w4_words, w4_scal
         interleave(on_vector, 2, 5)
         quantize_and_multiply(2, 4)
         quantize_and_multiply(2, 5)
-        x4_passes(1, 6, 8)
-        x4_passes(2, 6, 7)
-        scalar_relu(4)
-        scalar_relu(5)
+        x4_passes(1, 7, 8)
+        x4_passes(2, 6, 8)
+        for i in (4, 5):
+            for cols in halves:
+                scalar_relu(i, cols)
+            for cols in halves:
+                scalar_square(i, cols)
+            store(i, i + 1)
         interleave(on_vector, 0, 6)
         interleave(on_vector, 0, 7)
         quantize_and_multiply(0, 6)
@@ -221,12 +230,7 @@ def tile_mix_xres_tm_relu2_kernel(tc, x4_words, x4_scales, xr, w4_words, w4_scal
         interleave(on_vector, 2, 6)
         quantize_and_multiply(1, 6)
         quantize_and_multiply(2, 6)
-        x4_passes(2, 7, 8)
-        interleave(on_scalar, 1, 7)
-        scalar_square(4)
-        store(4, 5)
-        scalar_square(5)
-        store(5, 6)
+        interleave(on_vector, 1, 7)
         interleave(on_vector, 2, 7)
         quantize_and_multiply(1, 7)
         quantize_and_multiply(2, 7)

from contextlib import ExitStack

import concourse.mybir as mybir

K, T, N = 1536, 1024, 512
FLOPS = 2 * 2 * K * T * N

F32 = mybir.dt.float32
BF16 = mybir.dt.bfloat16
I32 = mybir.dt.int32
U32 = mybir.dt.uint32
U8 = mybir.dt.uint8
FP8X4 = mybir.dt.float8_e4m3fn_x4
FP4X4 = mybir.dt.float4_e2m1fn_x4
ACT = mybir.ActivationFunctionType

P = 128
PACK = 4
K_PASS = P * PACK
PASSES = K // K_PASS
LAST_PASS = PASSES - 1
TILES = T // P
QUADRANT = 32
SCALE_ROWS = 16
ALIGN = 256
WARM_UP_PASSES = 4

XR_LOADS = (
    (0, 0, 4), (1, 0, 4), (2, 0, 2), (2, 2, 4),
    (0, 4, 6), (1, 4, 6), (2, 4, 6),
    (0, 6, 8), (1, 6, 7), (2, 6, 7), (1, 7, 8), (2, 7, 8),
)


def tile_mix_xres_tm_relu2_kernel(tc, x4_words, x4_scales, xr, w4_words, w4_scales, out):
    nc = tc.nc
    with ExitStack() as ctx:
        keep = ctx.enter_context(tc.tile_pool(name="keep", bufs=1))
        psum = ctx.enter_context(tc.psum_pool(name="psum", bufs=1))
        ctx.enter_context(tc.manual_schedule())

        w4 = keep.tile([P, PASSES, 2 * N], U8, name="w4", align_bytes=ALIGN)
        w4_plane = keep.tile([P, PASSES, N], U8, name="w4_plane", align_bytes=ALIGN)
        x4 = keep.tile([P, PASSES, 2 * T], U8, name="x4", align_bytes=ALIGN)
        x4_plane = keep.tile([P, PASSES, T], U8, name="x4_plane", align_bytes=ALIGN)
        rounded = [keep.tile([P, T, PACK], BF16, name=f"rounded{a}", align_bytes=ALIGN) for a in range(PASSES)]
        codes = [keep.tile([P, T], U32, name=f"codes{a}", align_bytes=ALIGN) for a in range(PASSES)]
        xr_plane = [keep.tile([P, T], U8, name=f"xr_plane{a}", align_bytes=ALIGN) for a in range(PASSES)]
        positive = [keep.tile([P, N], F32, name=f"positive{i}", align_bytes=ALIGN) for i in range(TILES)]
        result = keep.tile([P, TILES, N], F32, name="result", align_bytes=ALIGN)
        table_probe = keep.tile([P, 1], F32, name="table_probe")
        acc = [psum.tile([P, N], F32, name=f"acc{i}") for i in range(TILES)]

        nc.vector.memset(w4_plane[:].rearrange("p a n -> p (a n)").bitcast(I32), 0)
        nc.vector.memset(x4_plane[:].rearrange("p a n -> p (a n)").bitcast(I32), 0)
        nc.gpsimd.memset(table_probe[:], 0.0)

        def load_words(tile, words, first_pass, end_pass):
            nc.sync.dma_start(
                out=tile[:, first_pass:end_pass, :].bitcast(I32),
                in_=words[first_pass:end_pass].rearrange("a p n -> p a n").bitcast(I32),
            )

        def load_scales(plane, scales, rows):
            for r in rows:
                nc.sync.dma_start(
                    out=plane[:].bitcast(I32)[r:P:QUADRANT, :, :],
                    in_=scales[:, r:SCALE_ROWS:4, :].rearrange("a g n -> g a n").bitcast(I32),
                )

        landed = {}

        def load_xr(a, first, end):
            raw = keep.tile([P, PACK, P * (end - first)], F32, name=f"raw{a}_{first}", align_bytes=ALIGN)
            rows = xr[K_PASS * a : K_PASS * (a + 1), P * first : P * end]
            nc.sync.dma_start(out=raw[:], in_=rows.rearrange("(p j) t -> p j t", j=PACK))
            for i in range(first, end):
                landed[a, i] = (raw, P * (i - first))

        on_vector, on_scalar = nc.vector.tensor_copy, nc.scalar.copy

        def interleave(copy, a, first, tiles=1):
            raw, t0 = landed[a, first]
            copy(
                out=rounded[a][:, P * first : P * (first + tiles), :].rearrange("p (c e) j -> p c j e", e=4),
                in_=raw[:, :, t0 : t0 + P * tiles].rearrange("p j (c e) -> p c j e", e=4),
            )

        def mx_pass(bank, a, lhsT, lhsT_scale, start, stop):
            nc.tensor.matmul_mx(
                out=bank[:],
                lhsT=lhsT,
                lhsT_scale=lhsT_scale,
                rhs=w4[:, a, :].bitcast(FP4X4),
                rhs_scale=w4_plane[:, a, :],
                start=start,
                stop=stop,
            )

        def x4_passes(a, first, end):
            for i in range(first, end):
                words = x4[:, a, 2 * P * i : 2 * P * (i + 1)].bitcast(FP4X4)
                mx_pass(acc[i], a, words, x4_plane[:, a, P * i : P * (i + 1)], start=(a == 0), stop=False)

        def quantize(a, first, tiles=1):
            cols = slice(P * first, P * (first + tiles))
            nc.vector.quantize_mx(
                out=codes[a][:, cols].bitcast(FP8X4),
                scales=xr_plane[a][:, cols],
                in_=rounded[a][:, cols, :].rearrange("p t j -> p (t j)"),
            )

        def xr_pass(a, i):
            cols = slice(P * i, P * (i + 1))
            mx_pass(acc[i], a, codes[a][:, cols].bitcast(FP8X4), xr_plane[a][:, cols], start=False, stop=(a == LAST_PASS))

        def quantize_and_multiply(a, first, tiles=1):
            quantize(a, first, tiles)
            for i in range(first, first + tiles):
                xr_pass(a, i)

        whole = slice(0, N)
        halves = [slice(h * N // 2, (h + 1) * N // 2) for h in range(2)]
        quarters = [slice(h * N // 4, (h + 1) * N // 4) for h in range(4)]

        def scalar_relu(i, cols=whole):
            nc.scalar.activation(out=positive[i][:, cols], in_=acc[i][:, cols], func=ACT.Relu)

        def scalar_square(i, cols=whole):
            nc.scalar.activation(out=result[:, i, cols], in_=positive[i][:, cols], func=ACT.Square)

        def vector_relu(i, cols):
            nc.vector.tensor_scalar_max(out=positive[i][:, cols], in0=acc[i][:, cols], scalar1=0.0)

        def vector_square(i, cols):
            nc.vector.tensor_mul(out=result[:, i, cols], in0=positive[i][:, cols], in1=positive[i][:, cols])

        def gpsimd_square(i, cols):
            nc.gpsimd.tensor_mul(out=result[:, i, cols], in0=positive[i][:, cols], in1=positive[i][:, cols])

        def store(first, end):
            rows = out[P * first : P * end, :].rearrange("(i p) n -> p i n", p=P)
            nc.sync.dma_start(out=rows, in_=result[:, first:end, :])

        nc.scalar.activation(out=table_probe[:], in_=table_probe[:], func=ACT.Relu)

        load_words(w4, w4_words, 0, PASSES)
        load_scales(w4_plane, w4_scales, range(0, 4))
        load_scales(x4_plane, x4_scales, range(0, 2))
        load_words(x4, x4_words, 0, PASSES)
        load_scales(x4_plane, x4_scales, range(2, 4))
        for a, first, end in XR_LOADS:
            load_xr(a, first, end)

        for repeat in range(WARM_UP_PASSES):
            mx_pass(acc[TILES - 1], 0, w4[:, 0, : 2 * P].bitcast(FP4X4), w4_plane[:, 0, :P], start=True, stop=True)

        x4_passes(0, 0, 4)
        x4_passes(1, 0, 4)
        x4_passes(2, 0, 4)
        x4_passes(0, 4, 5)
        interleave(on_vector, 0, 0)
        interleave(on_scalar, 0, 2)
        interleave(on_vector, 0, 1)
        interleave(on_scalar, 0, 3)
        quantize_and_multiply(0, 0)
        quantize_and_multiply(0, 1)
        quantize_and_multiply(0, 2)
        quantize_and_multiply(0, 3)
        x4_passes(0, 5, 6)
        x4_passes(1, 4, 5)
        interleave(on_vector, 1, 0)
        interleave(on_scalar, 1, 2)
        interleave(on_vector, 1, 1)
        interleave(on_scalar, 1, 3)
        quantize_and_multiply(1, 0)
        quantize_and_multiply(1, 1)
        quantize_and_multiply(1, 2)
        interleave(on_vector, 2, 0)
        quantize_and_multiply(1, 3)
        interleave(on_scalar, 2, 1)
        quantize_and_multiply(2, 0)
        quantize_and_multiply(2, 1)
        interleave(on_vector, 2, 2)
        interleave(on_scalar, 2, 3)
        quantize_and_multiply(2, 2)
        quantize_and_multiply(2, 3)
        x4_passes(1, 5, 6)
        x4_passes(2, 4, 6)
        x4_passes(0, 6, 7)
        scalar_relu(0)
        scalar_relu(1)
        scalar_square(0)
        store(0, 1)
        scalar_square(1)
        store(1, 2)
        scalar_relu(2)
        scalar_relu(3)
        scalar_square(2)
        store(2, 3)
        scalar_square(3)
        store(3, 4)
        interleave(on_vector, 0, 4)
        interleave(on_vector, 0, 5)
        quantize_and_multiply(0, 4)
        interleave(on_vector, 1, 4)
        quantize_and_multiply(0, 5)
        x4_passes(0, 7, 8)
        x4_passes(1, 6, 7)
        interleave(on_vector, 1, 5)
        quantize_and_multiply(1, 4)
        interleave(on_vector, 2, 4)
        quantize_and_multiply(1, 5)
        interleave(on_vector, 2, 5)
        quantize_and_multiply(2, 4)
        quantize_and_multiply(2, 5)
        x4_passes(1, 7, 8)
        x4_passes(2, 6, 8)
        for i in (4, 5):
            for cols in halves:
                scalar_relu(i, cols)
            for cols in halves:
                scalar_square(i, cols)
            store(i, i + 1)
        interleave(on_vector, 0, 6)
        interleave(on_vector, 0, 7)
        quantize_and_multiply(0, 6)
        interleave(on_vector, 1, 6)
        quantize_and_multiply(0, 7)
        interleave(on_vector, 2, 6)
        quantize_and_multiply(1, 6)
        quantize_and_multiply(2, 6)
        interleave(on_vector, 1, 7)
        interleave(on_vector, 2, 7)
        quantize_and_multiply(1, 7)
        quantize_and_multiply(2, 7)
        for cols in quarters:
            vector_relu(6, cols)
        for cols in quarters:
            scalar_square(6, cols)
        store(6, 7)
        for cols in quarters:
            vector_relu(7, cols)
        for h, square in enumerate((scalar_square, vector_square)):
            for cols in quarters[2 * h : 2 * h + 2]:
                square(7, cols)
        store(7, 8)
